import numpy as np, ml_dtypes
CORES = [1,5,17,21,33,37,49,53]
N = 8
BF = ml_dtypes.bfloat16
def gentries(a):
    return np.ascontiguousarray(a.reshape(8, 16, -1).transpose(0, 2, 1)).reshape(8, -1)
def gtable(e):
    e = np.asarray(e); return np.ascontiguousarray(e.reshape(8, -1, 16).transpose(0, 2, 1)).reshape(128, -1).astype(np.int32)
V, W, U, ND, G, K, B, H = 1408, 2048, 2, 1, 640, 2, 1, 2
KV, Q, TOPS, TH, FA, FB = K * V, 8, 2 ** 20 - 1, 7340025, 0.375, 0.625
def pick(t, c):
    return np.take_along_axis(t, c[:, None, :], 2)
def lend(t, sl):
    res = []
    for r in range(N):
        w = [t[r]]
        for e in range(ND):
            q = (r + e + 1) % N; w.append(pick(t[q], sl[q, :, e]))
        res.append(np.concatenate(w, axis=2))
    return np.stack(res)
def home(a, sl, both):
    res = []
    for q in range(N):
        o = a[q][:, :, :V]
        for e in range(ND):
            r = (q - e - 1) % N; b = np.zeros((8, 16, V), a.dtype)
            np.put_along_axis(b, sl[q, :, e][:, None, :], a[r][:, :, V + e * G:V + (e + 1) * G], 2)
            o = both(o, b)
        res.append(o)
    return np.stack(res)
def drop(z, x, both):
    b = np.zeros((8, 16, U * W), x.dtype)
    np.put_along_axis(b, z[:, None, :], x, 2)
    return both.reduce(b.reshape(8, 16, U, W), axis=2)
def coarse(cl, cr, snd, cu):
    c = cu & (W - 1); rule = np.repeat(cr, V, axis=4)
    t = lend(cl, snd[:, :, 0])
    s1 = np.stack([pick(t[r], c[r, :, 0, 0]) + pick(t[r], c[r, :, 0, 1]) + rule[r, :, :, 0] for r in range(N)])
    t = lend(np.maximum.reduce(s1.reshape(N, 8, 16, K, V), axis=3), snd[:, :, 1])
    s2, a = [], []
    for r in range(N):
        x, y = pick(t[r], c[r, :, 1, 0]), pick(t[r], c[r, :, 1, 1]); w = rule[r, :, :, 1]
        s2.append(x + y + w)
        a.append(np.maximum(drop(cu[r, :, 1, 0], y + w, np.maximum), drop(cu[r, :, 1, 1], x + w, np.maximum)))
    o = home(np.stack(a), snd[:, :, 1], np.maximum)
    return s1 + np.tile(o, (1, 1, 1, K)), np.stack(s2)
def parts(rng):
    d = {}
    d["cl"] = rng.integers(0, 2 ** 19, (N, 8, 1, V)) + rng.integers(0, 2 ** 19, (N, 8, 16, V))
    d["cr"] = rng.integers(0, 2 ** 19, (N, 8, 16, 2, K))
    d["cu"] = np.ascontiguousarray(np.argsort(rng.random((N, 8, 2, 2, U * W)), axis=-1)[..., :KV])
    d["fu"] = np.ascontiguousarray(np.argsort(rng.random((N, 8, 2, H, 2, U * W)), axis=-1)[..., :KV])
    d["snd"] = np.ascontiguousarray(np.argsort(rng.random((N, 8, 2, ND, V)), axis=-1)[..., :G])
    d["fl"] = 0.8 + 0.4 * rng.random((N, 8, 16, V))
    d["fw"] = FA + (FB - FA) * rng.random((N, 8, 16, 2, B * H))
    d["top"] = 0.5 + 1.5 * rng.random((N, 8, 16, V))
    return d
def bound(rng, p, lo, hi):
    s = np.sort(p[..., ::16], axis=-1); x = lo + (hi - lo) * rng.random((N, 8, 1, 1)) + 0.04 * rng.random((N, 8, 16, 1))
    return np.take_along_axis(s, (x * s.shape[-1]).astype(np.int64), 3)[..., 0]
def finish(rng, d, lo, hi):
    p = coarse(d["cl"], d["cr"], d["snd"], d["cu"])
    d["th"] = np.stack([bound(rng, p[0], lo, hi), bound(rng, p[1], lo, hi)], axis=-1)
    return d
def pack(d):
    e = {}
    for k in ("cl", "cr", "th"): e[k] = np.ascontiguousarray(d[k].reshape(N, 128, -1)).astype(np.int32)
    for k in ("cu", "fu", "snd"): e[k] = np.stack([gtable(a.reshape(8, -1)) for a in d[k]])
    e["fl"] = d["fl"].reshape(N, 128, V).astype(np.float32).astype(BF)
    e["fw"] = np.clip(d["fw"].reshape(N, 128, 2 * B * H), FA, FB).astype(np.float32)
    e["top"] = d["top"].reshape(N, 128, V).astype(np.float32).astype(BF)
    return e
def setup_inputs(rng):
    return pack(finish(rng, parts(rng), 0.4, 0.56))
def setup_inputs_brink(rng):
    d = parts(rng)
    d["cl"] = rng.integers(2 ** 19, 2 ** 20 - 8, (1, 8, 16, 1)) + rng.integers(0, 4, (N, 8, 16, V))
    d["cr"] = rng.integers(2 ** 19, 2 ** 20 - 8, (1, 8, 16, 1, 1)) + rng.integers(0, 2, (N, 8, 16, 2, K))
    return pack(finish(rng, d, 0.45, 0.56))
def crowd(rng, n):
    x = np.array([0, W - 1, V - 1, V]); o = np.concatenate([x, rng.permutation(np.setdiff1d(np.arange(W), x))])
    z = (o[:, None] + W * np.arange(U)[None, :]).reshape(-1)[:KV + KV // 8]
    return np.stack([rng.permutation(z)[:KV] for i in range(n)])
def setup_inputs_calm(rng):
    d = parts(rng); o = rng.permutation(8); full = o[0]; unit = 2.0 ** -10
    d["snd"] = np.ascontiguousarray(np.argsort(rng.random((N, 8, 2, V)), axis=-1)[..., :ND * G].reshape(N, 8, 2, ND, G))
    d["top"] = unit * (8 + 4 * rng.random((N, 8, 16, V)))
    d["top"][:, full] = unit * np.maximum(1.0, 0.75 + 0.5 * rng.random((N, 16, V)))
    kinds = ((0.25, 0.25, 0, 1), (0.25, 0.25, 1, 1), (0.05, 0.25, 1, 2), (0.02, 0.1, 1, 1))
    for i, (a, b, t1, t2) in enumerate(kinds):
        g = o[i + 1]
        d["cl"][:, g] = rng.random((N, 16, V)) < a
        d["cr"][:, g] = rng.random((N, 16, 2, K)) < b
        if i < 2:
            d["top"][:, g] = 0.5 * d["top"][:, g]
            for q in range(N):
                z = crowd(rng, 1)[0]; d["cu"][q, g, 1, 0] = z; d["cu"][q, g, 1, 1] = rng.permutation(z)
    d["snd"][:, full, :, :, 1:G - 1] = 1 + np.argsort(rng.random((N, 2, ND, V - 2)), axis=-1)[..., :G - 2]
    d["snd"][:, full, :, :, 0] = V - 1; d["snd"][:, full, :, :, G - 1] = 0
    e = V + G * np.arange(ND); most = np.concatenate([np.array([V - 1, 0]), e, e + G - 1])
    must = (most[:, None] + W * np.arange(U)[None, :]).reshape(-1); lack = W * (U - 1); rest = np.setdiff1d(np.arange(U * W), must)
    for q in range(N):
        for m in range(2):
            for h in range(H):
                for s in range(2):
                    first, last = must, must[:0]
                    if h == H - 1 and s == 1: first, last = must[must != lack], must[must == lack]
                    z = rng.permutation(rest); n = B * V - len(first); k = KV - B * V - len(last)
                    d["fu"][q, full, m, h, s] = np.concatenate([rng.permutation(np.concatenate([first, z[:n]])), rng.permutation(np.concatenate([last, z[n:n + k]]))])
    d = finish(rng, d, 0.4, 0.56); d["th"][:, full] = 0
    for i, (a, b, t1, t2) in enumerate(kinds):
        g = o[i + 1]
        for q in range(N):
            for m, t in enumerate((t1, t2)):
                d["th"][q, g, :, m] = t + 1; d["th"][q, g, rng.permutation(16)[:7], m] = t
    return pack(d)
def unused_felt(d, q, g):
    def uses(r):
        u = np.zeros(W, bool); u[d["cu"][r, g, 1] & (W - 1)] = True
        return u
    used = uses(q)[:V]
    for e in range(ND):
        s = d["snd"][q, g, 1, e]; used[s] = used[s] | uses((q - e - 1) % N)[V + e * G:V + (e + 1) * G]
    named = np.zeros(W, bool); named[d["fu"][q, g, 1][:, :, :B * V] & (W - 1)] = True
    return bool(np.any(named[:V] & ~used))
def setup_inputs_corners(rng):
    d = parts(rng); o = rng.permutation(8); few, full, rest = o[:2], o[2:4], o[4:]; lone = o[4]
    rest = rest[1:]
    d["snd"] = np.ascontiguousarray(np.argsort(rng.random((N, 8, 2, V)), axis=-1)[..., :ND * G].reshape(N, 8, 2, ND, G))
    d["top"] = 0.75 + 0.5 * rng.random((N, 8, 16, V)); d["top"][:, full] = d["top"][:, full] * 0.375
    for q in range(N):
        for g in few:
            d["cl"][q, g] = rng.integers(0, 1024, (16, V))
            for m in range(2):
                a = np.zeros(K, bool); i = int(rng.integers(0, 4))
                if i == 0: a[0] = True
                elif i == 1: a[K - 1] = True
                elif i == 2: a[:] = True
                else: a[1:] = True
                d["cr"][q, g, :, m] = np.where(a, TOPS, 0)
        for g in full:
            d["cu"][q, g] = crowd(rng, 4).reshape(2, 2, KV); d["fu"][q, g] = crowd(rng, 4 * H).reshape(2, H, 2, KV)
        g = full[0]; d["cu"][q, g, :, 1] = d["cu"][q, g, :, 0]; d["fu"][q, g, :, :, 1] = d["fu"][q, g, :, :, 0]
        d["cu"][q, lone, 1] = crowd(rng, 2)
    d = finish(rng, d, 0.4, 0.56); d["th"][:, few] = 5 * 2 ** 19
    for q in range(N):
        many, dead = 15 + q % 2, (Q - 1) * (1 - (q // 2) % 2)
        cases = ((many, many), (Q, Q), (Q, dead) if q % 2 == 0 else (dead, 16))
        for i, g in enumerate([lone] + list(rng.permutation(rest)[:2])):
            for m, n in enumerate(cases[i]):
                d["th"][q, g, :, m] = TH; d["th"][q, g, rng.permutation(16)[:n], m] = 0
    assert any(unused_felt(d, q, lone) for q in range(N))
    return pack(d)
def setup_inputs_ends(rng):
    d = parts(rng)
    col = rng.random((N, 8, 1, V)) < 0.85; flip = rng.random((N, 8, 16, V)) < 0.05
    d["cl"] = np.where(col ^ flip, TOPS, 0); d["cl"][..., V - 1] = TOPS; d["cl"][..., V - 2] = 0
    d["cr"] = np.where(rng.random((N, 8, 16, 2, K)) < 0.6, TOPS, 0); d["cr"][:, :, 15, :, K - 1] = TOPS
    th = np.full((N, 8, 16, 2), TH, np.int64)
    for g in range(8):
        i = rng.permutation(15); d["cl"][:, g, i[0]] = 0; d["cr"][:, g, i[0]] = 0
        for q in range(N):
            for m in range(2):
                n = 7 if g == 7 or q == N - 1 else int(rng.choice(np.array([6, 7, 7, 8])))
                th[q, g, i[:n], m] = 0
    d["th"] = th
    d["cr"][N - 1, 7, :, 1, 0] = np.minimum(d["cr"][N - 1, 7, :, 1, 0], TOPS - 1); d["cr"][N - 1, 7, 15, 1, 0] = TOPS - 1
    e = np.concatenate([np.arange(G // 2), np.arange(V - G // 2, V)]); d["snd"] = e[np.argsort(rng.random((N, 8, 2, ND, G)), axis=-1)]
    e = np.concatenate([np.arange(KV // 2), np.arange(U * W - KV // 2, U * W)])
    d["cu"] = e[np.argsort(rng.random((N, 8, 2, 2, KV)), axis=-1)]; d["fu"] = e[np.argsort(rng.random((N, 8, 2, H, 2, KV)), axis=-1)]
    d["fl"] = np.where(rng.random((N, 8, 16, V)) < 0.5, 0.75, 1.25)
    d["fw"] = np.where(rng.random((N, 8, 16, 2, B * H)) < 0.5, FA, FB)
    d["top"] = np.where(rng.random((N, 8, 16, V)) < 0.9, 32.0, 2.0 ** -10)
    return pack(d)
def setup_inputs_spread(rng):
    d = parts(rng)
    d["cl"] = np.minimum((np.exp2(20 * rng.random((N, 8, 1, V))) * (0.25 + 0.75 * rng.random((N, 8, 16, V)))).astype(np.int64), TOPS)
    d["cr"] = np.minimum(np.exp2(20 * rng.random((N, 8, 16, 2, K))).astype(np.int64), TOPS)
    d["fl"] = np.clip(0.75 + 0.5 * rng.random((N, 8, 1, V)) + 0.1 * (rng.random((N, 8, 16, V)) - 0.5), 0.75, 1.25)
    d["top"] = np.exp2(2 * rng.random((N, 8, 1, V)) - 1) * (0.75 + 0.5 * rng.random((N, 8, 16, V)))
    return pack(finish(rng, d, 0.4, 0.56))
def unlist(a, shape):
    return np.stack([gentries(x) for x in a]).astype(np.int64).reshape((N, 8) + shape)
def check_ranges(d):
    bad = []
    for k, lo, hi in (("cl", 0, TOPS), ("cr", 0, TOPS), ("th", 0, TH), ("cu", 0, U * W - 1), ("fu", 0, U * W - 1), ("snd", 0, V - 1)):
        if np.min(d[k]) < lo or np.max(d[k]) > hi: bad.append("range of " + k)
    for k, lo, hi in (("fl", 0.75, 1.25), ("fw", FA, FB), ("top", 2.0 ** -10, 32.0)):
        x = np.asarray(d[k]).astype(np.float64)
        if not np.all((x >= lo) & (x <= hi)): bad.append("range of " + k)
    for k, n in (("cu", KV), ("fu", KV), ("snd", G)):
        s = np.sort(unlist(d[k], (-1, n)), axis=-1)
        if np.any(s[..., 1:] == s[..., :-1]): bad.append("repeated numbers in a block of " + k)
    return bad
def reference(cl, cr, th, cu, fu, snd, fl, fw, top):
    sl = unlist(snd, (2, ND, G)); cz = unlist(cu, (2, 2, KV)); fz = unlist(fu, (2, H, 2, KV)); fc = fz & (W - 1)
    p = coarse(cl.astype(np.int64).reshape(N, 8, 16, V), cr.astype(np.int64).reshape(N, 8, 16, 2, K), sl, cz)
    t = th.astype(np.int64).reshape(N, 8, 16, 2)
    counted, place = [], []
    for m in range(2):
        votes = np.add.reduce((p[m] >= t[:, :, :, m:m + 1]).astype(np.int64), axis=2)
        live = (votes >= Q).astype(np.int64).reshape(N, 8, K, V)
        before = np.add.accumulate(live, axis=2) - live
        counted.append(((live == 1) & (before < B)).reshape(N, 8, KV)); place.append(np.minimum(before, B - 1).reshape(N, 8, KV))
    wts = fw.astype(np.float64).reshape(N, 8, 16, 2, B * H)
    def weight(r, m, h):
        return pick(wts[r, :, :, m], place[m][r] * H + h) * counted[m][r][:, None, :]
    x = fl.astype(np.float64).reshape(N, 8, 16, V); known = []
    for m in range(2):
        known.append(lend(x, sl[:, :, m])); res = []
        for r in range(N):
            y = np.zeros((8, 16, V))
            for h in range(H):
                e = pick(known[m][r], fc[r, :, m, h, 0]) * pick(known[m][r], fc[r, :, m, h, 1]) * weight(r, m, h)
                y = y + np.add.reduce(e.reshape(8, 16, K, V), axis=2)
            res.append(y)
        x = np.stack(res)
    o = top.astype(np.float64).reshape(N, 8, 16, V)
    for m in (1, 0):
        res = []
        for r in range(N):
            a = np.zeros((8, 16, W))
            for h in range(H):
                e = np.tile(o[r], (1, 1, K)) * weight(r, m, h)
                a = a + drop(fz[r, :, m, h, 0], e * pick(known[m][r], fc[r, :, m, h, 1]), np.add) + drop(fz[r, :, m, h, 1], e * pick(known[m][r], fc[r, :, m, h, 0]), np.add)
            res.append(a)
        o = home(np.stack(res), sl[:, :, m], np.add)
    return {"yi": x.reshape(N, 128, V).astype(np.float32), "yo": o.reshape(N, 128, V).astype(np.float32)}

def check_inputs(d):
    bad = list(check_ranges(d))
    if not bad:
        for name, y in reference(**d).items():
            for q in range(N):
                v = np.abs(np.asarray(y[q], np.float64)); s = np.sqrt(np.mean(v * v))
                if v.max() > 15 * s or s < 2.0 ** -10: bad.append('%s of rank %d is uneven or too small' % (name, q))
    return bad

@@ -1,0 +1,523 @@
+from concourse.mybir import dt, AluOpType as ALU, ActivationFunctionType as ACT
+
+V, GH, KV, W = 1408, 640, 2816, 2048
+SL = 1424
+NSL = 15
+ZC = 16
+XC = 32
+KS = float(2 ** 24)
+
+SCRATCH = {
+    "w0": ("sbuf", [128, 4096], "float32"), "w1": ("sbuf", [128, 4096], "float32"),
+    "w2": ("sbuf", [128, 4096], "float32"), "w3": ("sbuf", [128, 4096], "float32"),
+    "pool": ("sbuf", [128, NSL * SL], "float32"),
+    "t0": ("sbuf", [128, W], "float32"), "t1": ("sbuf", [128, W], "float32"),
+    "tf0": ("sbuf", [128, W + ZC], "bfloat16"), "tf1": ("sbuf", [128, W + ZC], "float32"),
+    "cli": ("sbuf", [128, V], "int32"), "cui": ("sbuf", [128, 704], "int32"), "cm": ("sbuf", [128, 704], "int32"),
+    "fz0": ("sbuf", [128, 704], "int32"), "fz1": ("sbuf", [128, 704], "int32"), "dz": ("sbuf", [128, 704], "float32"),
+    "sni": ("sbuf", [128, 80], "int32"), "cri": ("sbuf", [128, 4], "int32"), "thi": ("sbuf", [128, 4], "int32"),
+    "fwf": ("sbuf", [128, 4], "float32"), "col": ("sbuf", [128, 32], "float32"),
+    "sn16": ("sbuf", [128, 80], "uint16"), "cu16": ("sbuf", [128, 704], "uint16"), "pm16": ("sbuf", [128, 352], "uint16"),
+    "invf": ("sbuf", [128, 768], "float32"), "inv16": ("sbuf", [128, 512], "uint16"),
+    "c16": ("sbuf", [128, 704], "uint16"), "z16": ("sbuf", [128, 704], "uint16"),
+    "sm": ("sbuf", [128, 448], "float32"),
+    "land": ("sbuf", [128, 3 * GH], "float32"), "gs": ("sbuf", [128, 4 * GH], "float32"), "gfl": ("sbuf", [128, GH], "bfloat16"),
+    "bits": ("sbuf", [128, 2 * KV], "bfloat16"),
+    "ident": ("sbuf", [128, 256], "float32"), "band": ("sbuf", [128, 2 * 160], "bfloat16"), "bsrc": ("sbuf", [128, 16], "bfloat16"),
+    "ps": ("psum", [128, 4096], "float32"),
+}
+DMAS = ["snd", "cub", "cua", "cl", "cr", "fl", "fu", "fw", "top", "exl", "exr", "exs", "za", "zc", "rz", "yia", "yib", "yic", "yo"]
+SEMAPHORES = ["cv", "cs", "cp", "cg"] + ["d" + n for n in DMAS] + ["arr%d" % i for i in range(7)] + ["snt%d" % i for i in range(7)]
+
+SAME_QUEUE_OVERWRITE_WAITS = True
+W0V, W0S = 2048, 640
+PRE_L = 1248
+RV = 1792
+XV = 1760
+YH = 704
+CH1 = 352
+CHF = 704
+YH1 = 768
+SPLIT, THREE2, THREE1, PE2, PE1, PEF, PEC, ZG = True, False, False, True, True, False, True, False
+
+
+def rank_program(g, core, T, topo):
+    rank = T.rank_of(core)
+    if rank is None:
+        return
+    n = len(T.cores)
+    down, up = T.cores[(rank - 1) % n], T.cores[(rank + 1) % n]
+    Q = {"v": g.vector, "s": g.scalar, "p": g.tensor, "g": g, "y": g.sync}
+    CNT = {"v": "cv", "s": "cs", "p": "cp", "g": "cg"}
+    total, known, log = {}, {q: {} for q in Q}, {}
+
+    def ap(r):
+        if len(r) == 4:
+            return T[r[0]][:, r[1]:r[2]:r[3]]
+        return T[r[0]][:, r[1]:r[2]]
+
+    def need(q, reads, writes):
+        toks = {}
+        for rs, wr in ((reads, False), (writes, True)):
+            for r in rs:
+                for (lo, hi, w, eng, sem, val) in log.get(r[0], []):
+                    hit = lo < r[2] and r[1] < hi
+                    if eng == q:
+                        must = hit and ((w and not wr) or (SAME_QUEUE_OVERWRITE_WAITS and q != "p" and (w or wr)))
+                    elif r[0] == "ps":
+                        must = lo // 512 <= (r[2] - 1) // 512 and r[1] // 512 <= (hi - 1) // 512
+                    else:
+                        lo4, hi4 = lo // 8 * 8, (hi + 7) // 8 * 8
+                        must = (hit and (w or wr)) or (w and wr and lo4 < r[2] and r[1] < hi4)
+                    if must:
+                        toks[sem] = max(toks.get(sem, 0), val)
+        for sem, val in toks.items():
+            if known[q].get(sem, 0) < val:
+                Q[q].wait_ge(T.sem[sem], val)
+                known[q][sem] = val
+
+    def note(eng, reads, writes, sem, val):
+        for rs, wr in ((reads, False), (writes, True)):
+            for r in rs:
+                log.setdefault(r[0], []).append((r[1], r[2], wr, eng, sem, val))
+
+    def op(q, call, reads, writes):
+        need(q, reads, writes)
+        sem = CNT[q]
+        total[sem] = total.get(sem, 0) + 1
+        call().then_inc(T.sem[sem], 1)
+        note(q, reads, writes, sem, total[sem])
+
+    def dmas(q, name, items, **kw):
+        sem = "d" + name
+        for it in items:
+            need(q, it[2], it[3])
+        for it in items:
+            Q[q].dma_start(it[0], it[1], **kw).then_inc(T.sem[sem], 16)
+        total[sem] = 16 * len(items)
+        for it in items:
+            note("dma", it[2], it[3], sem, total[sem])
+
+    def after(q, sem):
+        if known[q].get(sem, 0) < total[sem]:
+            Q[q].wait_ge(T.sem[sem], total[sem])
+            known[q][sem] = total[sem]
+
+    def exchange(i, src, dst, to, frm):
+        need("g", [src], [])
+        rid, pid, _se = topo.addr(to)
+        g.remote_dma(ap(dst), ap(src), T.sem["arr%d" % i], T.sem["snt%d" % i], pid, rid, topo.mask(core, to))
+        total["snt%d" % i] = len(topo.engines(core, to))
+        total["arr%d" % i] = len(topo.engines(frm, core))
+        note("dma", [src], [], "snt%d" % i, total["snt%d" % i])
+        note("dma", [], [dst], "arr%d" % i, total["arr%d" % i])
+
+    def sub(r, a, b):
+        return (r[0], r[1] + a, r[1] + b)
+
+    def slot(i, a=0, b=V):
+        return ("pool", i * SL + a, i * SL + b)
+
+    def cl_(x):
+        return ap(x) if isinstance(x, tuple) else x
+
+    def rd(*xs):
+        return [x for x in xs if isinstance(x, tuple)]
+
+    def ind(win, off):
+        return ap(win).indirect(ap(off))
+
+    def vcopy(o, i):
+        op("v", lambda: g.vector.tensor_copy(ap(o), ap(i)), [i], [o])
+
+    def vset(o, c):
+        op("v", lambda: g.vector.memset(ap(o), c), [], [o])
+
+    def vts(o, i, s1, o0, s2=None, o1=None, off=None):
+        src = (lambda: ap(i)) if off is None else (lambda: ind(i, off))
+        if o1 is None:
+            op("v", lambda: g.vector.tensor_scalar(ap(o), src(), cl_(s1), None, o0), rd(i, s1, off), [o])
+        else:
+            op("v", lambda: g.vector.tensor_scalar(ap(o), src(), cl_(s1), cl_(s2), o0, o1), rd(i, s1, s2, off), [o])
+
+    def vtt(o, a, b, alu):
+        op("v", lambda: g.vector.tensor_tensor(ap(o), ap(a), ap(b), alu), [a, b], [o])
+
+    def vgather(o, win, off):
+        op("v", lambda: g.vector.tensor_copy(ap(o), ind(win, off)), [win, off], [o])
+
+    def vgt(o, win, off, b, alu):
+        op("v", lambda: g.vector.tensor_tensor(ap(o), ind(win, off), ap(b), alu), [win, off, b], [o])
+
+    def vscat(win, off, i):
+        op("v", lambda: g.vector.tensor_copy(ind(win, off), ap(i)), [i, off], [win])
+
+    def vst(win, off, a, b, alu):
+        op("v", lambda: g.vector.tensor_tensor(ind(win, off), ap(a), ap(b), alu), [a, b, off], [win])
+
+    def act(o, i, off=None, bias=None, scale=None, func=None):
+        kw = {}
+        if bias is not None:
+            kw["bias"] = cl_(bias)
+        if scale is not None:
+            kw["scale"] = cl_(scale)
+        f = func if func is not None else (ACT.Copy if bias is None else ACT.Identity)
+        src = (lambda: ap(i)) if off is None else (lambda: ind(i, off))
+        op("s", lambda: g.scalar.activation(ap(o), src(), f, **kw), rd(i, off, bias, scale), [o])
+
+    def sscat(win, off, i):
+        op("s", lambda: g.scalar.activation(ind(win, off), ap(i), ACT.Silu), [i, off], [win])
+
+    def gfill(o, step=0, base=0):
+        op("g", lambda: g.iota(ap(o), [[step, o[2] - o[1]]], base, 0, allow_small_or_imprecise_dtypes=True), [], [o])
+
+    def mm(o, lhs, rhs, start, stop):
+        op("p", lambda: g.tensor.matmul(ap(o), ap(lhs), ap(rhs), start, stop), [lhs, rhs], [o])
+
+    def zero_by_dma(name, ws, src):
+        dmas("y", name, [(ap(sub(w, a, a + 2048)), ap(sub(src, 0, 2048)), [sub(src, 0, 2048)], [sub(w, a, a + 2048)])
+                         for w in ws for a in (0, 2048)])
+
+    WL, WR, WA2, WB2 = (("w%d" % i, 0, 4096) for i in range(4))
+    WA1, WB1 = WL, WR
+    T0, T1, TF0, TF1 = ("t0", 0, W), ("t1", 0, W), ("tf0", 0, W + ZC), ("tf1", 0, W + ZC)
+    SN0, SN1 = ("sn16", 0, 40), ("sn16", 40, 80)
+    PX, PY, PG = ("ps", 0, V), ("ps", 1536, 1536 + V), ("ps", 3072, 3072 + GH)
+    PV0, PV1 = ("ps", 3072, 3160), ("ps", 3584, 3672)
+    G0, G1, G2, G3 = (("gs", i * GH, (i + 1) * GH) for i in range(4))
+    LAND = [("land", i * GH, (i + 1) * GH) for i in range(3)]
+    col = lambda i: ("col", i, i + 1)
+    CR, TH, SG, WA, W2 = 0, 4, 8, 12, 16
+    fwc = lambda i: ("fwf", i, i + 1)
+    IOTA, AL, S1 = slot(0, 0, KV), slot(2, 0, KV), slot(4, 0, KV)
+    X, Y, OC, OM, TOP = slot(6, 0, KV + XC), slot(8, 0, KV + XC), slot(10), slot(11), slot(14)
+    ID, IDS = ("ident", 0, 128), ("ident", 128, 256)
+    cuts = [(a, min(V, a + 512)) for a in range(0, V, 512)]
+    cul = lambda m, s, a, b: ("cu16", (m * 2 + s) * 176 + a // 16, (m * 2 + s) * 176 + b // 16)
+    fl_ = lambda name, m, h, s, a=0, b=V: (name, ((m * 2 + h) * 2 + s) * 88 + a // 16, ((m * 2 + h) * 2 + s) * 88 + b // 16)
+
+    dmas("y", "snd", [(T.sni[:], T.snd[:], [], [("sni", 0, 80)])])
+    dmas("y", "cl", [(T.cli[:], T.cl[:], [], [("cli", 0, V)])])
+    dmas("s", "cub", [(T.cui[:, 352:704], T.cu[:, 352:704], [], [("cui", 352, 704)])])
+    dmas("s", "cua", [(T.cui[:, 0:352], T.cu[:, 0:352], [], [("cui", 0, 352)])])
+    dmas("s", "cr", [(T.cri[:], T.cr[:], [], [("cri", 0, 4)]), (T.thi[:, 0:2], T.th[:], [], [("thi", 0, 2)])])
+    dmas("y", "fw", [(T.fwf[:], T.fw[:], [], [("fwf", 0, 4)])])
+    dmas("y", "fu", [(T["fz%d" % k][:, l * 88:(l + 1) * 88], T.fu[:, l * 176 + k * 88:l * 176 + (k + 1) * 88], [],
+                      [("fz%d" % k, l * 88, (l + 1) * 88)]) for l in range(8) for k in range(2)])
+    dmas("y", "fl", [(T.tf0[:, ZC:ZC + V], T.fl[:], [], [("tf0", ZC, ZC + V)])])
+
+    gfill(sub(IOTA, 0, 352), 1, XC)
+    gfill(sub(WL, W0V + W0S, 4096))
+    vset(sub(WL, 0, W0V), 0.0)
+    act(sub(IOTA, 352, 704), sub(IOTA, 0, 352), bias=352.0)
+    act(sub(IOTA, 704, V), sub(IOTA, 0, 704), bias=704.0)
+    act(sub(IOTA, V, KV), sub(IOTA, 0, V), bias=1408.0)
+    act(sub(WL, W0V, W0V + W0S), sub(WL, 0, W0S))
+
+    vts(("cm", 352, 704), ("cui", 352, 704), 4097.0, ALU.mult)
+    vts(("cm", 0, 352), ("cm", 352, 704), 4, ALU.logical_shift_right, 4095, ALU.bitwise_and)
+    vcopy(("sn16", 0, 80), ("sni", 0, 80))
+    vcopy(("pm16", 0, 352), ("cm", 0, 352))
+    vgather(G0, ("cli", 0, V), SN0)
+    exchange(0, G0, sub(T0, V, W), down, up)
+    gfill(sub(WR, 0, 2048))
+    gfill(sub(WR, 2048, 4096))
+    after("y", "snt0")
+    zero_by_dma("za", [WA2], WR)
+    sscat(WL, ("pm16", 0, PRE_L // 16), sub(IOTA, 0, PRE_L))
+    vcopy(sub(T0, 0, V), ("cli", 0, V))
+    vts(("cm", 0, 704), ("cui", 0, 704), W - 1, ALU.bitwise_and)
+    vcopy(("col", CR, CR + 4), ("cri", 0, 4))
+    vcopy(("col", TH, TH + 2), ("thi", 0, 2))
+    vcopy(("cu16", 0, 704), ("cm", 0, 704))
+    vts(("col", SG + 2, SG + 4), ("col", CR + 2, CR + 4), col(TH + 1), ALU.add)
+    vts(("col", WA, WA + 2), ("fwf", 0, 2), 1.0 / KS, ALU.mult)
+    vts(("col", W2, W2 + 2), ("fwf", 2, 4), KS * KS, ALU.mult)
+    vset(("tf0", 0, ZC), 0.0)
+    vset(("tf1", 0, ZC), 0.0)
+    vset(sub(X, 0, XC), 0.0)
+    vset(sub(Y, 0, XC), 0.0)
+    vset(("band", 0, 320), 0.0)
+    vset(("bsrc", 0, 8), 4096.0)
+    vts(("col", SG, SG + 2), ("col", SG + 2, SG + 4), -1.0, ALU.mult, 0.5, ALU.add)
+    act(("gfl", 0, GH), ("tf0", ZC, ZC + V), off=SN0)
+    exchange(3, ("gfl", 0, GH), sub(TF0, ZC + V, ZC + W), down, up)
+    vtt(("dz", 0, 704), ("fz0", 0, 704), ("fz1", 0, 704), ALU.subtract)
+
+    for a, b in ((0, CH1), (CH1, 3 * CH1), (3 * CH1, V), (V, V + 2 * CH1), (V + 2 * CH1, KV)):
+        if a == 0:
+            vts(sub(AL, a, b), T0, col(CR), ALU.add, off=cul(0, 0, a, b))
+        else:
+            act(sub(AL, a, b), T0, off=cul(0, 0, a, b), bias=col(CR + a // V))
+        vgt(sub(S1, a, b), T0, cul(0, 1, a, b), sub(AL, a, b), ALU.add)
+    act(G2, sub(S1, 0, V), off=SN1)
+    vgt(G1, sub(S1, V, KV), SN1, G2, ALU.max)
+    exchange(1, G1, sub(T1, V, W), down, up)
+    sscat(WL, ("pm16", PRE_L // 16, 176), sub(IOTA, PRE_L, KV))
+    dmas("y", "exl", [(T.invf[:, 0:256], T.w0[0:128:18, :], [WL], [("invf", 0, 256)])])
+    vtt(sub(T1, 0, V), sub(S1, 0, V), sub(S1, V, KV), ALU.max)
+    vscat(WR, ("pm16", 176, 176 + RV // 16), sub(IOTA, 0, RV))
+    sscat(WA2, ("pm16", 176 + RV // 16, 352), sub(IOTA, RV, KV))
+    dmas("y", "exs", [(T.invf[:, 512:768], T.w2[0:128:18, :], [WA2], [("invf", 512, 768)])])
+    dmas("y", "exr", [(T.invf[:, 256:512], T.w1[0:128:18, :], [WR], [("invf", 256, 512)])])
+
+    gfill(ID, 0, 1)
+    op("g", lambda: g.affine_select(ap(ID), ap(ID), [[-1, 128]], ALU.is_equal, 0.0, 0, 1), [ID], [ID])
+    op("g", lambda: g.affine_select(T.bsrc[:, 8:16], T.bsrc[:, 0:8], [[-16, 8]], ALU.is_ge, 0.0, 0, 1), [("bsrc", 0, 8)], [("bsrc", 8, 16)])
+    for j in range(2):
+        o = ("band", 160 * j + 16 + j, 160 * j + 16 + j + 113, 16)
+        op("g", lambda o=o: g.affine_select(ap(o), T.bsrc[:, 8:16], [[16, 8]], ALU.is_ge, 0.0, 15, -1), [("bsrc", 8, 16)], [o])
+    dmas("g", "top", [(ap(TOP), T.top[:], [], [TOP])])
+    gfill(WB2)
+
+    def votes(m, k, out):
+        for i in range(16):
+            j = i % 2
+            a = 160 * j + 16 + j - i
+            b0 = m * KV + k * V
+            mm(out, ("band", a, a + 128), ("bits", b0 + i, b0 + V - 15 + i, 16), i == 0, i == 15)
+
+    def lists_first(m, thr, off):
+        c0 = m * 352
+        vts(PV0, PV0, thr, ALU.is_ge)
+        for l in range(4):
+            vtt(("sm", l * 88, l * 88 + 88), ("dz", c0 + l * 88, c0 + l * 88 + 88), PV0, ALU.mult)
+        vts(("sm", 352, 440), PV0, 65536.0, ALU.mult, off, ALU.add)
+
+    def lists_places(m):
+        c0 = m * 352
+        vtt(("cm", 0, 352), ("sm", 0, 352), ("fz1", c0, c0 + 352), ALU.add)
+        vts(("cm", 352, 704), ("cm", 0, 352), W - 1, ALU.bitwise_and)
+
+    def lists_second(m):
+        c0 = m * 352
+        vtt(PV1, PV1, ("sm", 352, 440), ALU.add)
+        for l in range(4):
+            vtt(("sm", l * 88, l * 88 + 88), ("cm", 352 + l * 88, 440 + l * 88), PV1, ALU.min)
+        vts(("c16", c0, c0 + 352), ("sm", 0, 352), float(ZC), ALU.add)
+
+    def psum(acc, lhs, x, start, stop):
+        for a in range(0, x[2] - x[1], 512):
+            b = min(x[2] - x[1], a + 512)
+            mm(sub(acc, a, b), lhs, sub(x, a, b), start, stop)
+
+    def sum2(k):
+        if PEC:
+            psum(PY, ID, sub(Y, XC + k * V, XC + (k + 1) * V), True, False)
+            psum(PY, ID, sub(X, XC + k * V, XC + (k + 1) * V), False, True)
+
+    def sign2(k):
+        if PEC:
+            act(("bits", KV + k * V, KV + (k + 1) * V), PY, bias=col(SG + k), func=ACT.Sign)
+        else:
+            act(PY, sub(Y, XC + k * V, XC + (k + 1) * V), bias=col(SG + 2 + k), scale=-1.0)
+
+    def cmp2(k):
+        if not PEC:
+            vtt(("bits", KV + k * V, KV + (k + 1) * V), sub(X, XC + k * V, XC + (k + 1) * V), PY, ALU.is_ge)
+
+    vts(("inv16", 0, 256), ("invf", 0, 256), 0.25, ALU.add)
+    for k in range(2):
+        act(sub(Y, XC + k * V, XC + (k + 1) * V), T1, off=cul(1, 1, k * V, (k + 1) * V), bias=col(CR + 2 + k))
+    act(G2, Y, off=("inv16", 88, 128))
+    cut = KV - XV
+    for a, b in ((0, min(cut, V)), (V, cut)):
+        if b > a:
+            act(sub(X, XC + a, XC + b), T1, off=cul(1, 0, a, b), bias=col(CR + 2 + a // V))
+    for a, b in ((cut, V), (max(cut, V), KV)):
+        if b > a:
+            vts(sub(X, XC + a, XC + b), T1, col(CR + 2 + a // V), ALU.add, off=cul(1, 0, a, b))
+    vtt(("invf", 256, 512), ("invf", 256, 512), ("invf", 512, 768), ALU.add)
+    vgt(G2, Y, ("inv16", 216, 256), G2, ALU.max)
+    vts(("inv16", 256, 512), ("invf", 256, 512), 0.25, ALU.add)
+    vgt(G2, X, ("inv16", 256 + 88, 256 + 128), G2, ALU.max)
+    vgt(G2, X, ("inv16", 256 + 216, 512), G2, ALU.max)
+    exchange(2, G2, LAND[0], up, down)
+    sum2(0)
+    act(OM, Y, off=("inv16", 0, 88))
+    act(OC, Y, off=("inv16", 128, 216))
+    act(G0, OC, off=SN1)
+    gfill(WA2)
+    after("y", "snt2")
+    zero_by_dma("rz", [WL, WR], WB2)
+    vgt(OM, X, ("inv16", 256, 256 + 88), OM, ALU.max)
+    vgt(OM, X, ("inv16", 256 + 128, 256 + 216), OM, ALU.max)
+    act(PX, OM)
+    vst(OC, SN1, G0, LAND[0], ALU.max)
+
+    for a, b in cuts:
+        vtt(sub(PX, a, b), sub(OC, a, b), sub(PX, a, b), ALU.max)
+        act(sub(PX, a, b), sub(PX, a, b), bias=col(TH), scale=-1.0)
+    for a, b in cuts:
+        vtt(("bits", a, b), sub(S1, a, b), sub(PX, a, b), ALU.is_ge)
+    votes(0, 0, PV0)
+    vtt(("bits", V, KV), sub(S1, V, KV), PX, ALU.is_ge)
+    votes(0, 1, PV1)
+    E0, E1 = slot(0), slot(1)
+    sign2(0)
+    act(E0, TOP, scale=col(W2))
+    act(E1, TOP, scale=col(W2 + 1))
+    lists_first(0, 32767.0, -30720.0)
+    if PEC:
+        votes(1, 0, PV0)
+        sum2(1)
+    lists_places(0)
+    lists_second(0)
+    if PEC:
+        lists_first(1, 0.0, 2048.0)
+    else:
+        cmp2(0)
+        votes(1, 0, PV0)
+
+    A = [slot(2), slot(3)]
+    B = [slot(10), slot(11)]
+    P = [slot(12), slot(13)]
+    for h in range(2):
+        for a in range(0, V, CHF):
+            act(sub(A[h], a, a + CHF), TF0, off=fl_("c16", 0, h, 0, a, a + CHF), scale=col(WA + h))
+            vgt(sub(P[h], a, a + CHF), TF0, fl_("c16", 0, h, 1, a, a + CHF), sub(A[h], a, a + CHF), ALU.mult)
+        if h == 0 and PEF:
+            psum(PX, ID, P[0], True, False)
+    act(G0, P[0], off=SN1)
+    vgt(G1, P[1], SN1, G0, ALU.add)
+    exchange(4, G1, sub(TF1, ZC + V, ZC + W), down, up)
+    sign2(1)
+    if PEC:
+        votes(1, 1, PV1)
+    if PEF:
+        psum(PX, ID, P[1], False, True)
+        act(B[0], TF0, off=fl_("c16", 0, 0, 1), scale=fwc(0))
+        act(sub(TF1, ZC, ZC + V), PX)
+    else:
+        act(PX, P[0])
+        act(B[0], TF0, off=fl_("c16", 0, 0, 1), scale=fwc(0))
+    vcopy(("z16", 0, 352), ("cm", 0, 352))
+    if not PEC:
+        cmp2(1)
+        votes(1, 1, PV1)
+        lists_first(1, 32767.0, -30720.0)
+    lists_places(1)
+    if not PEF:
+        vtt(sub(TF1, ZC, ZC + V), P[1], PX, ALU.add)
+    lists_second(1)
+    vcopy(("z16", 352, 704), ("cm", 0, 352))
+    if not THREE2:
+        act(PY, TOP)
+    act(IDS, ID, scale=1.0 / KS)
+
+    GA = [slot(4), slot(5)]
+    VB1, VB2, VR, RA, VA = slot(6), slot(7), slot(8), slot(9), slot(12)
+    O1, YA, YB = slot(13), slot(0), slot(1)
+    halves = lambda w, a, b: [sub(w, a, b), sub(w, W + a, W + b)]
+
+    def late(acc, lhs, w, start):
+        for a, b in cuts:
+            mm(sub(acc, a, b), lhs, sub(w, a, b), start, False)
+            mm(sub(acc, a, b), lhs, sub(w, W + a, W + b), False, True)
+
+    def chain(acc, terms, out, parts):
+        for a, b in parts:
+            for x in terms[:-1]:
+                vtt(sub(acc, a, b), sub(x, a, b), sub(acc, a, b), ALU.add)
+            vtt(sub(out, a, b), sub(terms[-1], a, b), sub(acc, a, b), ALU.add)
+
+    two = [(0, 1024), (1024, V)] if SPLIT else [(0, V)]
+    vgt(VB1, TF1, fl_("c16", 1, 0, 1), E0, ALU.mult)
+    act(GA[0], TF1, off=fl_("c16", 1, 0, 0), scale=col(W2))
+    if THREE2:
+        WC2 = WA1
+        sscat(WB2, fl_("z16", 1, 0, 0), VB1)
+        vst(WA2, fl_("z16", 1, 0, 1), TOP, GA[0], ALU.mult)
+        vgt(VB2, TF1, fl_("c16", 1, 1, 1), E1, ALU.mult)
+        act(RA, WA2, off=fl_("z16", 1, 1, 1))
+        sscat(WC2, fl_("z16", 1, 1, 0), VB2)
+        vgt(VA, TF1, fl_("c16", 1, 1, 0), E1, ALU.mult)
+        vst(WA2, fl_("z16", 1, 1, 1), RA, VA, ALU.add)
+        psum(PG, ID, sub(WB2, V, W), True, False)
+        psum(PG, ID, sub(WB2, W + V, 2 * W), False, True)
+        psum(PX, ID, sub(WB2, 0, V), True, False)
+        psum(PX, ID, sub(WB2, W, W + V), False, False)
+        late(PX, ID, WC2, False)
+        chain(PG, halves(WC2, V, W) + halves(WA2, V, W), G3, [(0, GH)])
+        exchange(5, G3, LAND[1], up, down)
+        gfill(WA1)
+        act(GA[1], TF1, off=fl_("c16", 1, 1, 0), scale=col(W2 + 1))
+        own2 = halves(WA2, 0, V)
+    else:
+        vgt(VB2, TF1, fl_("c16", 1, 1, 1), E1, ALU.mult)
+        sscat(WB2, fl_("z16", 1, 0, 0), VB1)
+        vst(WA2, fl_("z16", 1, 0, 1), TOP, GA[0], ALU.mult)
+        act(GA[1], TF1, off=fl_("c16", 1, 1, 0), scale=col(W2 + 1))
+        vgt(VR, WB2, fl_("z16", 1, 1, 0), VB2, ALU.add)
+        act(RA, WA2, off=fl_("z16", 1, 1, 1))
+        vtt(VA, GA[1], PY, ALU.mult)
+        sscat(WB2, fl_("z16", 1, 1, 0), VR)
+        vst(WA2, fl_("z16", 1, 1, 1), RA, VA, ALU.add)
+        act(PG, sub(WB2, V, W))
+        chain(PG, halves(WA2, V, W) + [sub(WB2, W + V, 2 * W)], G3, [(0, GH)])
+        exchange(5, G3, LAND[1], up, down)
+        if PE2:
+            late(PX, ID, WB2, True)
+            own2 = halves(WA2, 0, V)
+        else:
+            act(PX, sub(WB2, 0, V))
+            own2 = halves(WA2, 0, V) + [sub(WB2, W, W + V)]
+    WC1 = WB2
+    act(PY, B[0])
+    act(B[1], TF0, off=fl_("c16", 0, 1, 1), scale=fwc(1))
+    if YH:
+        vgt(sub(YA, 0, YH), TF1, fl_("c16", 1, 0, 1, 0, YH), sub(GA[0], 0, YH), ALU.mult)
+    chain(PX, own2, O1, two)
+    if THREE1 and ZG:
+        gfill(WC1)
+    elif THREE1:
+        after("y", "snt5")
+        zero_by_dma("zc", [WC1], WB1)
+    act(G0, O1, off=SN1)
+    vgt(sub(YA, YH, V), TF1, fl_("c16", 1, 0, 1, YH, V), sub(GA[0], YH, V), ALU.mult)
+    dmas("y", "yia", [(T.yi[:], ap(YA), [YA], [("yi", 0, V)])])
+    vst(O1, SN1, G0, LAND[1], ALU.add)
+
+    O0 = slot(14)
+    vtt(VB1, O1, PY, ALU.mult)
+    act(PX, O1)
+    sscat(WB1, fl_("z16", 0, 0, 0), VB1)
+    vst(WA1, fl_("z16", 0, 0, 1), O1, A[0], ALU.mult)
+    vtt(VB2, B[1], PX, ALU.mult)
+    act(RA, WA1, off=fl_("z16", 0, 1, 1))
+    if THREE1:
+        sscat(WC1, fl_("z16", 0, 1, 0), VB2)
+        last = WC1
+        psum(PG, IDS, sub(WB1, V, W), True, False)
+        psum(PG, IDS, sub(WB1, W + V, 2 * W), False, True)
+        psum(PY, IDS, sub(WB1, 0, V), True, False)
+        psum(PY, IDS, sub(WB1, W, W + V), False, not PE1)
+    else:
+        vgt(VR, WB1, fl_("z16", 0, 1, 0), VB2, ALU.add)
+        sscat(WB1, fl_("z16", 0, 1, 0), VR)
+        last = WB1
+    vtt(VA, A[1], PX, ALU.mult)
+    vst(WA1, fl_("z16", 0, 1, 1), RA, VA, ALU.add)
+    act(G2 if THREE1 else PG, sub(last, V, W), scale=1.0 / KS)
+    act(G3, sub(last, W + V, 2 * W), scale=1.0 / KS)
+    own1 = halves(WA1, 0, V)
+    if PE1:
+        late(PY, IDS, last, not THREE1)
+    else:
+        act(VR if THREE1 else PY, sub(last, 0, V), scale=1.0 / KS)
+        act(VB1, sub(last, W, W + V), scale=1.0 / KS)
+        own1 = own1 + ([VR] if THREE1 else []) + [VB1]
+    chain(PG, halves(WA1, V, W) + ([G2] if THREE1 else []) + [G3], G1, [(0, GH)])
+    exchange(6, G1, LAND[2], up, down)
+    if YH1:
+        vgt(sub(YB, 0, YH1), TF1, fl_("c16", 1, 1, 1, 0, YH1), sub(GA[1], 0, YH1), ALU.mult)
+        dmas("g", "yib", [(T.yi[:, 0:YH1], ap(sub(YB, 0, YH1)), [sub(YB, 0, YH1)], [("yi", 0, YH1)])], accum_op=ALU.add)
+    chain(PY, own1, O0, two)
+    act(G0, O0, off=SN0)
+    if YH1 < V:
+        vgt(sub(YB, YH1, V), TF1, fl_("c16", 1, 1, 1, YH1, V), sub(GA[1], YH1, V), ALU.mult)
+        dmas("g", "yic", [(T.yi[:, YH1:V], ap(sub(YB, YH1, V)), [sub(YB, YH1, V)], [("yi", YH1, V)])], accum_op=ALU.add)
+    vst(O0, SN0, G0, LAND[2], ALU.add)
+    dmas("y", "yo", [(T.yo[:], ap(O0), [O0], [("yo", 0, V)])])
+    for sem in total:
+        after("g", sem)

@@ -5,6 +5,7 @@ SL = 1424
 NSL = 15
 ZC = 16
 XC = 32
+LW = XC + GH
 KS = float(2 ** 24)
 
 SCRATCH = {
@@ -14,31 +15,38 @@ SCRATCH = {
     "t0": ("sbuf", [128, W], "float32"), "t1": ("sbuf", [128, W], "float32"),
     "tf0": ("sbuf", [128, W + ZC], "bfloat16"), "tf1": ("sbuf", [128, W + ZC], "float32"),
     "cli": ("sbuf", [128, V], "int32"), "cui": ("sbuf", [128, 704], "int32"), "cm": ("sbuf", [128, 704], "int32"),
-    "fz0": ("sbuf", [128, 704], "int32"), "fz1": ("sbuf", [128, 704], "int32"), "dz": ("sbuf", [128, 704], "float32"),
+    "fz": ("sbuf", [128, V], "int32"), "dz": ("sbuf", [128, 704], "float32"),
     "sni": ("sbuf", [128, 80], "int32"), "cri": ("sbuf", [128, 4], "int32"), "thi": ("sbuf", [128, 4], "int32"),
+    "snm": ("sbuf", [128, 160], "int32"),
     "fwf": ("sbuf", [128, 4], "float32"), "col": ("sbuf", [128, 32], "float32"),
-    "sn16": ("sbuf", [128, 80], "uint16"), "cu16": ("sbuf", [128, 704], "uint16"), "pm16": ("sbuf", [128, 352], "uint16"),
-    "invf": ("sbuf", [128, 768], "float32"), "inv16": ("sbuf", [128, 512], "uint16"),
+    "sn16": ("sbuf", [128, 160], "uint16"), "cu16": ("sbuf", [128, 704], "uint16"), "pm16": ("sbuf", [128, 352], "uint16"),
+    "invf": ("sbuf", [128, 768], "float32"), "inv16": ("sbuf", [128, 704], "uint16"),
     "c16": ("sbuf", [128, 704], "uint16"), "z16": ("sbuf", [128, 704], "uint16"),
-    "sm": ("sbuf", [128, 448], "float32"),
-    "land": ("sbuf", [128, 3 * GH], "float32"), "gs": ("sbuf", [128, 4 * GH], "float32"), "gfl": ("sbuf", [128, GH], "bfloat16"),
+    "sm": ("sbuf", [128, 448], "float32"), "zs": ("sbuf", [128, 256], "float32"),
+    "land": ("sbuf", [128, 3 * LW], "float32"), "gs": ("sbuf", [128, 3 * GH], "float32"), "gfl": ("sbuf", [128, GH], "bfloat16"),
     "bits": ("sbuf", [128, 2 * KV], "bfloat16"),
     "ident": ("sbuf", [128, 256], "float32"), "band": ("sbuf", [128, 2 * 160], "bfloat16"), "bsrc": ("sbuf", [128, 16], "bfloat16"),
     "ps": ("psum", [128, 4096], "float32"),
 }
-DMAS = ["snd", "cub", "cua", "cl", "cr", "fl", "fu", "fw", "top", "exl", "exr", "exs", "za", "zc", "rz", "yia", "yib", "yic", "yo"]
+DMAS = ["snd", "cul", "cur", "cua", "cl", "cr", "fl", "fu", "fw", "top", "zl", "zr", "z1", "z0", "exl", "exr", "ex1", "ex0",
+        "add", "yia", "yib"] + ["yo%d" % i for i in range(6)]
 SEMAPHORES = ["cv", "cs", "cp", "cg"] + ["d" + n for n in DMAS] + ["arr%d" % i for i in range(7)] + ["snt%d" % i for i in range(7)]
 
-SAME_QUEUE_OVERWRITE_WAITS = True
-W0V, W0S = 2048, 640
-PRE_L = 1248
-RV = 1792
-XV = 1760
-YH = 704
-CH1 = 352
-CHF = 704
-YH1 = 768
-SPLIT, THREE2, THREE1, PE2, PE1, PEF, PEC, ZG = True, False, False, True, True, False, True, False
+ZV = 2048
+PRE_S = 2112
+PRE_V = 1120
+RV = 1920
+YV, XV = 1408, 1408
+RBS = 1056
+EARLY = True
+YS = 896
+WHOLE, HALVES = ((0, GH),), ((0, GH // 2), (GH // 2, GH))
+PARTS = [WHOLE, WHOLE, HALVES, WHOLE, WHOLE, HALVES, HALVES]
+HOMEC = [(0, 192), (192, 512), (512, 960), (960, 1408)]
+L1A = 352
+HOME1 = [(0, 352, "v"), (352, 704, "s"), (704, 1056, "s"), (1056, 1408, "s")]
+SC1 = [(0, 352), (352, 704), (704, 1408)]
+HOME0 = [(0, 192, "s"), (192, 608, "s"), (608, 1024, "s"), (1024, 1408, "s")]
 
 
 def rank_program(g, core, T, topo):
@@ -63,7 +71,7 @@ def rank_program(g, core, T, topo):
                 for (lo, hi, w, eng, sem, val) in log.get(r[0], []):
                     hit = lo < r[2] and r[1] < hi
                     if eng == q:
-                        must = hit and ((w and not wr) or (SAME_QUEUE_OVERWRITE_WAITS and q != "p" and (w or wr)))
+                        must = hit and ((w and not wr) or (q != "p" and (w or wr)))
                     elif r[0] == "ps":
                         must = lo // 512 <= (r[2] - 1) // 512 and r[1] // 512 <= (hi - 1) // 512
                     else:
@@ -98,17 +106,21 @@ def rank_program(g, core, T, topo):
         for it in items:
             note("dma", it[2], it[3], sem, total[sem])
 
+    def load(q, name, o, src):
+        dmas(q, name, [(ap(o), src, [], [o])])
+
     def after(q, sem):
         if known[q].get(sem, 0) < total[sem]:
             Q[q].wait_ge(T.sem[sem], total[sem])
             known[q][sem] = total[sem]
 
-    def exchange(i, src, dst, to, frm):
-        need("g", [src], [])
+    def exchange(i, src, dst, to, frm, parts=((0, GH),)):
         rid, pid, _se = topo.addr(to)
-        g.remote_dma(ap(dst), ap(src), T.sem["arr%d" % i], T.sem["snt%d" % i], pid, rid, topo.mask(core, to))
-        total["snt%d" % i] = len(topo.engines(core, to))
-        total["arr%d" % i] = len(topo.engines(frm, core))
+        for a, b in parts:
+            need("g", [sub(src, a, b)], [])
+            g.remote_dma(ap(sub(dst, a, b)), ap(sub(src, a, b)), T.sem["arr%d" % i], T.sem["snt%d" % i], pid, rid, topo.mask(core, to))
+        total["snt%d" % i] = len(parts) * len(topo.engines(core, to))
+        total["arr%d" % i] = len(parts) * len(topo.engines(frm, core))
         note("dma", [src], [], "snt%d" % i, total["snt%d" % i])
         note("dma", [], [dst], "arr%d" % i, total["arr%d" % i])
 
@@ -174,101 +186,186 @@ def rank_program(g, core, T, topo):
     def mm(o, lhs, rhs, start, stop):
         op("p", lambda: g.tensor.matmul(ap(o), ap(lhs), ap(rhs), start, stop), [lhs, rhs], [o])
 
-    def zero_by_dma(name, ws, src):
-        dmas("y", name, [(ap(sub(w, a, a + 2048)), ap(sub(src, 0, 2048)), [sub(src, 0, 2048)], [sub(w, a, a + 2048)])
-                         for w in ws for a in (0, 2048)])
+    def pesum(acc, lhs, xs):
+        width = xs[0][2] - xs[0][1]
+        for a in range(0, width, 512):
+            b = min(width, a + 512)
+            for j, x in enumerate(xs):
+                mm(sub(acc, a, b), lhs, sub(x, a, b), j == 0, j == len(xs) - 1)
+
+    ONE = (slice(0, 128, 18), slice(14, 126, 14))
+
+    def zero_one(name, win, s):
+        z = ("zs", 0, (win[2] - win[1]) // 16)
+        dmas("y", name, [(T[win[0]][ONE[s], win[1]:win[2]], ap(z), [z], [win])])
+
+    def deal(name, tile, win, s):
+        dmas("y", name, [(ap(tile), T[win[0]][ONE[s], win[1]:win[2]], [win], [tile])])
 
     WL, WR, WA2, WB2 = (("w%d" % i, 0, 4096) for i in range(4))
     WA1, WB1 = WL, WR
     T0, T1, TF0, TF1 = ("t0", 0, W), ("t1", 0, W), ("tf0", 0, W + ZC), ("tf1", 0, W + ZC)
-    SN0, SN1 = ("sn16", 0, 40), ("sn16", 40, 80)
-    PX, PY, PG = ("ps", 0, V), ("ps", 1536, 1536 + V), ("ps", 3072, 3072 + GH)
-    PV0, PV1 = ("ps", 3072, 3160), ("ps", 3584, 3672)
-    G0, G1, G2, G3 = (("gs", i * GH, (i + 1) * GH) for i in range(4))
-    LAND = [("land", i * GH, (i + 1) * GH) for i in range(3)]
+    WS1, WS0 = sub(WA2, 0, W), T0
+    SN0, SN1, PM0, PM1 = (("sn16", 40 * i, 40 * i + 40) for i in range(4))
+    PA, PB, PG = ("ps", 0, V), ("ps", 1536, 1536 + V), ("ps", 3072, 3072 + GH)
+    PV0, PV1, PT = ("ps", 3072, 3160), ("ps", 3584, 3672), ("ps", 3200, 3552)
+    G0, G1, G2 = (("gs", i * GH, (i + 1) * GH) for i in range(3))
+    LAND = [("land", i * LW, (i + 1) * LW) for i in range(3)]
     col = lambda i: ("col", i, i + 1)
     CR, TH, SG, WA, W2 = 0, 4, 8, 12, 16
-    fwc = lambda i: ("fwf", i, i + 1)
+    W0, RC, RT = 20, 24, 28
     IOTA, AL, S1 = slot(0, 0, KV), slot(2, 0, KV), slot(4, 0, KV)
     X, Y, OC, OM, TOP = slot(6, 0, KV + XC), slot(8, 0, KV + XC), slot(10), slot(11), slot(14)
     ID, IDS = ("ident", 0, 128), ("ident", 128, 256)
-    cuts = [(a, min(V, a + 512)) for a in range(0, V, 512)]
+    banks = [(a, min(V, a + 512)) for a in range(0, V, 512)]
     cul = lambda m, s, a, b: ("cu16", (m * 2 + s) * 176 + a // 16, (m * 2 + s) * 176 + b // 16)
     fl_ = lambda name, m, h, s, a=0, b=V: (name, ((m * 2 + h) * 2 + s) * 88 + a // 16, ((m * 2 + h) * 2 + s) * 88 + b // 16)
+    inv = lambda s, a, b: ("inv16", s * 256 + a // 16, s * 256 + b // 16)
+    home = lambda m, a, b: ("inv16", 512 + m * 96 + a // 16, 512 + m * 96 + b // 16)
+    half = lambda w, j: sub(w, j * W, (j + 1) * W)
 
-    dmas("y", "snd", [(T.sni[:], T.snd[:], [], [("sni", 0, 80)])])
-    dmas("y", "cl", [(T.cli[:], T.cl[:], [], [("cli", 0, V)])])
-    dmas("s", "cub", [(T.cui[:, 352:704], T.cu[:, 352:704], [], [("cui", 352, 704)])])
-    dmas("s", "cua", [(T.cui[:, 0:352], T.cu[:, 0:352], [], [("cui", 0, 352)])])
-    dmas("s", "cr", [(T.cri[:], T.cr[:], [], [("cri", 0, 4)]), (T.thi[:, 0:2], T.th[:], [], [("thi", 0, 2)])])
-    dmas("y", "fw", [(T.fwf[:], T.fw[:], [], [("fwf", 0, 4)])])
-    dmas("y", "fu", [(T["fz%d" % k][:, l * 88:(l + 1) * 88], T.fu[:, l * 176 + k * 88:l * 176 + (k + 1) * 88], [],
-                      [("fz%d" % k, l * 88, (l + 1) * 88)]) for l in range(8) for k in range(2)])
-    dmas("y", "fl", [(T.tf0[:, ZC:ZC + V], T.fl[:], [], [("tf0", ZC, ZC + V)])])
-
+    load("s", "snd", ("sni", 0, 80), T.snd[:])
+    load("y", "cul", ("cui", 352, 528), T.cu[:, 352:528])
+    load("y", "cl", ("cli", 0, V), T.cl[:])
+    load("s", "cur", ("cui", 528, 704), T.cu[:, 528:704])
+    load("s", "cua", ("cui", 0, 352), T.cu[:, 0:352])
+    dmas("s", "cr", [(T.cri[:], T.cr[:], [], [("cri", 0, 4)]), (T.thi[:, 0:2], T.th[:], [], [("thi", 0, 2)]),
+                     (T.fwf[:], T.fw[:], [], [("fwf", 0, 4)])])
     gfill(sub(IOTA, 0, 352), 1, XC)
-    gfill(sub(WL, W0V + W0S, 4096))
-    vset(sub(WL, 0, W0V), 0.0)
-    act(sub(IOTA, 352, 704), sub(IOTA, 0, 352), bias=352.0)
-    act(sub(IOTA, 704, V), sub(IOTA, 0, 704), bias=704.0)
-    act(sub(IOTA, V, KV), sub(IOTA, 0, V), bias=1408.0)
-    act(sub(WL, W0V, W0V + W0S), sub(WL, 0, W0S))
+    vset(("zs", 0, 256), 0.0)
+    zero_one("zr", WR, 1)
+    zero_one("z1", WS1, 0)
+    gfill(sub(IOTA, 704, V), 1, XC + 704)
+    gfill(sub(IOTA, V, KV), 1, XC + V)
+    vset(sub(WL, 0, ZV), 0.0)
+    act(sub(IOTA, 352, 704), sub(IOTA, 0, 352), bias=352.0, func=ACT.Silu)
+    act(sub(WL, 3072, 4096), sub(WL, 0, 1024))
 
-    vts(("cm", 352, 704), ("cui", 352, 704), 4097.0, ALU.mult)
-    vts(("cm", 0, 352), ("cm", 352, 704), 4, ALU.logical_shift_right, 4095, ALU.bitwise_and)
+    def dealt(out, src, tmp, bits):
+        k = src[2] - src[1]
+        vts(sub(tmp, 0, k), src, float(2 ** (bits + 4) + 1), ALU.mult)
+        vts(sub(tmp, k, 2 * k), sub(tmp, 0, k), 4, ALU.logical_shift_right, 2 ** (bits + 4) - 1, ALU.bitwise_and)
+        vcopy(out, sub(tmp, k, 2 * k))
+
     vcopy(("sn16", 0, 80), ("sni", 0, 80))
-    vcopy(("pm16", 0, 352), ("cm", 0, 352))
-    vgather(G0, ("cli", 0, V), SN0)
-    exchange(0, G0, sub(T0, V, W), down, up)
-    gfill(sub(WR, 0, 2048))
-    gfill(sub(WR, 2048, 4096))
-    after("y", "snt0")
-    zero_by_dma("za", [WA2], WR)
-    sscat(WL, ("pm16", 0, PRE_L // 16), sub(IOTA, 0, PRE_L))
+    dealt(("pm16", 0, 176), ("cui", 352, 528), ("cm", 0, 352), 8)
+    vset(sub(WL, ZV, 3072), 0.0)
+    vset(ID, 1.0)
+    for a, b in PARTS[0]:
+        vgather(sub(G0, a, b), ("cli", 0, V), sub(SN0, a // 16, b // 16))
+    exchange(0, G0, sub(T0, V, W), down, up, PARTS[0])
+    op("g", lambda: g.affine_select(ap(ID), ap(ID), [[-1, 128]], ALU.is_equal, 0.0, 0, 1), [ID], [ID])
+    for x in [("tf0", 0, ZC), ("tf1", 0, ZC), sub(X, 0, XC), sub(Y, 0, XC), ("band", 0, 320)] + [sub(x, 0, XC) for x in LAND]:
+        gfill(x)
+    gfill(("bsrc", 0, 8), 0, 4096)
+    gfill(half(WB2, 0))
+    dmas("g", "top", [(ap(TOP), T.top[:], [], [TOP])])
+    if not EARLY:
+        after("y", "snt0")
+    load("y", "fu", ("fz", 0, V), T.fu[:])
+    load("y", "fl", ("tf0", ZC, ZC + V), T.fl[:])
+    sscat(WL, ("pm16", 0, 88), sub(IOTA, 0, V))
+    if PRE_S > V:
+        sscat(WL, ("pm16", 88, PRE_S // 16), sub(IOTA, V, PRE_S))
+    dealt(("pm16", 176, 352), ("cui", 528, 704), ("cm", 352, 704), 8)
     vcopy(sub(T0, 0, V), ("cli", 0, V))
-    vts(("cm", 0, 704), ("cui", 0, 704), W - 1, ALU.bitwise_and)
+    vts(("cm", 0, 352), ("cui", 0, 352), W - 1, ALU.bitwise_and)
     vcopy(("col", CR, CR + 4), ("cri", 0, 4))
     vcopy(("col", TH, TH + 2), ("thi", 0, 2))
-    vcopy(("cu16", 0, 704), ("cm", 0, 704))
+    vcopy(("cu16", 0, 352), ("cm", 0, 352))
+    dealt(("sn16", 80, 160), ("sni", 0, 80), ("snm", 0, 160), 7)
+    op("v", lambda: g.vector.reciprocal(ap(("col", RC, RC + 2)), T.fwf[:, 0:3:2]), [("fwf", 0, 4)], [("col", RC, RC + 2)])
     vts(("col", SG + 2, SG + 4), ("col", CR + 2, CR + 4), col(TH + 1), ALU.add)
-    vts(("col", WA, WA + 2), ("fwf", 0, 2), 1.0 / KS, ALU.mult)
-    vts(("col", W2, W2 + 2), ("fwf", 2, 4), KS * KS, ALU.mult)
-    vset(("tf0", 0, ZC), 0.0)
-    vset(("tf1", 0, ZC), 0.0)
-    vset(sub(X, 0, XC), 0.0)
-    vset(sub(Y, 0, XC), 0.0)
-    vset(("band", 0, 320), 0.0)
-    vset(("bsrc", 0, 8), 4096.0)
+    vts(("col", WA, WA + 2), ("fwf", 0, 2), KS, ALU.mult)
+    vts(col(W0), ("fwf", 0, 1), 1.0 / KS, ALU.mult)
+    vts(("col", W2, W2 + 2), ("fwf", 2, 4), 1.0 / (KS * KS), ALU.mult)
     vts(("col", SG, SG + 2), ("col", SG + 2, SG + 4), -1.0, ALU.mult, 0.5, ALU.add)
-    act(("gfl", 0, GH), ("tf0", ZC, ZC + V), off=SN0)
-    exchange(3, ("gfl", 0, GH), sub(TF0, ZC + V, ZC + W), down, up)
-    vtt(("dz", 0, 704), ("fz0", 0, 704), ("fz1", 0, 704), ALU.subtract)
+    vts(col(RT), ("fwf", 1, 2), col(RC), ALU.mult, KS * KS, ALU.mult)
+    vts(col(RT + 1), ("fwf", 3, 4), col(RC + 1), ALU.mult)
+    vscat(WR, ("pm16", 176, 176 + PRE_V // 16), sub(IOTA, 0, PRE_V))
 
-    for a, b in ((0, CH1), (CH1, 3 * CH1), (3 * CH1, V), (V, V + 2 * CH1), (V + 2 * CH1, KV)):
+    for a, b in ((0, L1A), (L1A, 704), (704, V), (V, V + 704), (V + 704, KV)):
         if a == 0:
             vts(sub(AL, a, b), T0, col(CR), ALU.add, off=cul(0, 0, a, b))
         else:
             act(sub(AL, a, b), T0, off=cul(0, 0, a, b), bias=col(CR + a // V))
         vgt(sub(S1, a, b), T0, cul(0, 1, a, b), sub(AL, a, b), ALU.add)
+        if b == V:
+            pesum(PA, ID, [sub(S1, 0, V)])
     act(G2, sub(S1, 0, V), off=SN1)
-    vgt(G1, sub(S1, V, KV), SN1, G2, ALU.max)
-    exchange(1, G1, sub(T1, V, W), down, up)
-    sscat(WL, ("pm16", PRE_L // 16, 176), sub(IOTA, PRE_L, KV))
-    dmas("y", "exl", [(T.invf[:, 0:256], T.w0[0:128:18, :], [WL], [("invf", 0, 256)])])
-    vtt(sub(T1, 0, V), sub(S1, 0, V), sub(S1, V, KV), ALU.max)
-    vscat(WR, ("pm16", 176, 176 + RV // 16), sub(IOTA, 0, RV))
-    sscat(WA2, ("pm16", 176 + RV // 16, 352), sub(IOTA, RV, KV))
-    dmas("y", "exs", [(T.invf[:, 512:768], T.w2[0:128:18, :], [WA2], [("invf", 512, 768)])])
-    dmas("y", "exr", [(T.invf[:, 256:512], T.w1[0:128:18, :], [WR], [("invf", 256, 512)])])
-
-    gfill(ID, 0, 1)
-    op("g", lambda: g.affine_select(ap(ID), ap(ID), [[-1, 128]], ALU.is_equal, 0.0, 0, 1), [ID], [ID])
+    for a, b in PARTS[1]:
+        vgt(sub(G1, a, b), sub(S1, V, KV), sub(SN1, a // 16, b // 16), sub(G2, a, b), ALU.max)
+    exchange(1, G1, sub(T1, V, W), down, up, PARTS[1])
     op("g", lambda: g.affine_select(T.bsrc[:, 8:16], T.bsrc[:, 0:8], [[-16, 8]], ALU.is_ge, 0.0, 0, 1), [("bsrc", 0, 8)], [("bsrc", 8, 16)])
     for j in range(2):
         o = ("band", 160 * j + 16 + j, 160 * j + 16 + j + 113, 16)
         op("g", lambda o=o: g.affine_select(ap(o), T.bsrc[:, 8:16], [[16, 8]], ALU.is_ge, 0.0, 15, -1), [("bsrc", 8, 16)], [o])
-    dmas("g", "top", [(ap(TOP), T.top[:], [], [TOP])])
-    gfill(WB2)
+    gfill(half(WB2, 1))
+    gfill(half(WA2, 1))
+    vscat(WR, ("pm16", 176 + PRE_V // 16, 176 + RV // 16), sub(IOTA, PRE_V, RV))
+    if PRE_S < KV:
+        sscat(WL, ("pm16", PRE_S // 16, 176), sub(IOTA, PRE_S, KV))
+    deal("exl", ("invf", 0, 256), WL, 0)
+    sscat(WS1, PM1, sub(IOTA, 0, GH))
+    if RV < KV:
+        sscat(WR, ("pm16", 176 + RV // 16, 352), sub(IOTA, RV, KV))
+    deal("exr", ("invf", 256, 512), WR, 1)
+    deal("ex1", ("invf", 512, 640), WS1, 0)
+    zero_one("z0", WS0, 1)
+    vts(("cm", 352, 704), ("cui", 352, 704), W - 1, ALU.bitwise_and)
+    vtt(sub(T1, 0, V), sub(S1, V, KV), PA, ALU.max)
+    vcopy(("cu16", 352, 704), ("cm", 352, 704))
+    fz = lambda l, k: ("fz", l * 176 + k * 88, l * 176 + k * 88 + 88)
+
+    def differences(m):
+        for l in range(4 * m, 4 * m + 4):
+            vtt(("dz", l * 88, l * 88 + 88), fz(l, 0), fz(l, 1), ALU.subtract)
+
+    differences(0)
+
+    def children(tab, s, nv):
+        for a, b in ((0, min(V, KV - nv)), (V, KV - nv)):
+            if b > a:
+                act(sub(tab, XC + a, XC + b), T1, off=cul(1, s, a, b), bias=col(CR + 2 + a // V))
+        for a, b in ((KV - nv, V), (max(KV - nv, V), KV)):
+            if b > a:
+                vts(sub(tab, XC + a, XC + b), T1, col(CR + 2 + a // V), ALU.add, off=cul(1, s, a, b))
+
+    vts(inv(0, 0, 4096), ("invf", 0, 256), 0.25, ALU.add)
+    children(Y, 1, YV)
+    act(G2, Y, off=inv(0, V, W))
+    children(X, 0, XV)
+    vgt(G2, Y, inv(0, W + V, 2 * W), G2, ALU.max)
+    vts(inv(1, 0, 4096), ("invf", 256, 512), 0.25, ALU.add)
+    for a, b in PARTS[2]:
+        for u in (V, W + V):
+            vgt(sub(G2, a, b), X, inv(1, u + a, u + b), sub(G2, a, b), ALU.max)
+    exchange(2, G2, sub(LAND[0], XC, LW), up, down, PARTS[2])
+    pesum(PB, ID, [sub(Y, XC, XC + V), sub(X, XC, XC + V)])
+
+    E1, H = slot(1), slot(12)
+    act(OM, Y, off=inv(0, 0, V))
+    act(OC, Y, off=inv(0, W, W + V), bias=col(TH), scale=-1.0)
+    act(("gfl", 0, GH), ("tf0", ZC, ZC + V), off=SN0)
+    exchange(3, ("gfl", 0, GH), sub(TF0, ZC + V, ZC + W), down, up)
+    vgt(OM, X, inv(1, 0, V), OM, ALU.max)
+    vts(home(1, 0, V), ("invf", 512, 600), 0.25, ALU.add)
+    for a, b in banks:
+        vgt(sub(OM, a, b), X, inv(1, W + a, W + b), sub(OM, a, b), ALU.max)
+    XK1, YK1 = sub(X, XC + V, XC + KV), sub(Y, XC + V, XC + KV)
+    dmas("g", "add", [(ap(XK1), ap(YK1), [XK1, YK1], [XK1])], accum_op=ALU.add)
+    gfill(half(WA2, 0))
+    for a, b in banks:
+        act(sub(PA, a, b), sub(OM, a, b), bias=col(TH), scale=-1.0)
+    for a, b in banks:
+        vtt(sub(PA, a, b), sub(OC, a, b), sub(PA, a, b), ALU.min)
+    for a, b in HOMEC:
+        act(sub(H, a, b), LAND[0], off=home(1, a, b), bias=col(TH), scale=-1.0)
+    for j in range(len(HOMEC) + 1):
+        if j < len(HOMEC):
+            vtt(sub(PA, *HOMEC[j]), sub(H, *HOMEC[j]), sub(PA, *HOMEC[j]), ALU.min)
+        if j > 0:
+            vtt(sub(("bits", 0, V), *HOMEC[j - 1]), sub(S1, *HOMEC[j - 1]), sub(PA, *HOMEC[j - 1]), ALU.is_ge)
 
     def votes(m, k, out):
         for i in range(16):
@@ -277,247 +374,152 @@ def rank_program(g, core, T, topo):
             b0 = m * KV + k * V
             mm(out, ("band", a, a + 128), ("bits", b0 + i, b0 + V - 15 + i, 16), i == 0, i == 15)
 
-    def lists_first(m, thr, off):
+    def lists(m, off):
         c0 = m * 352
-        vts(PV0, PV0, thr, ALU.is_ge)
+        four = lambda name, l, a=0, k=1: (name, a + l * 88, a + (l + k) * 88)
         for l in range(4):
-            vtt(("sm", l * 88, l * 88 + 88), ("dz", c0 + l * 88, c0 + l * 88 + 88), PV0, ALU.mult)
-        vts(("sm", 352, 440), PV0, 65536.0, ALU.mult, off, ALU.add)
-
-    def lists_places(m):
-        c0 = m * 352
-        vtt(("cm", 0, 352), ("sm", 0, 352), ("fz1", c0, c0 + 352), ALU.add)
-        vts(("cm", 352, 704), ("cm", 0, 352), W - 1, ALU.bitwise_and)
-
-    def lists_second(m):
-        c0 = m * 352
-        vtt(PV1, PV1, ("sm", 352, 440), ALU.add)
+            vtt(four("ps", l, PT[1]), four("dz", m * 4 + l), PV0, ALU.mult)
+        vts(four("sm", 4), PV0, 65536.0, ALU.mult, off, ALU.add)
         for l in range(4):
-            vtt(("sm", l * 88, l * 88 + 88), ("cm", 352 + l * 88, 440 + l * 88), PV1, ALU.min)
-        vts(("c16", c0, c0 + 352), ("sm", 0, 352), float(ZC), ALU.add)
+            vtt(four("cm", l), fz(m * 4 + l, 1), four("ps", l, PT[1]), ALU.add)
+        vts(four("cm", 4, 0, 2), four("cm", 0, 0, 2), W - 1, ALU.bitwise_and)
+        vtt(PV1, four("sm", 4), PV1, ALU.add)
+        vts(four("cm", 6, 0, 2), four("cm", 2, 0, 2), W - 1, ALU.bitwise_and)
+        for l in range(4):
+            vtt(four("sm", l), four("cm", 4 + l), PV1, ALU.min)
+            if l == 1:
+                vts(four("c16", 0, c0), four("sm", 0), float(ZC), ALU.add)
+        vts(four("c16", 1, c0), four("sm", 1), float(ZC), ALU.add)
+        vcopy(("z16", c0, c0 + 352), ("cm", 0, 352))
+        vts(four("c16", 2, c0, 2), four("sm", 2, 0, 2), float(ZC), ALU.add)
 
-    def psum(acc, lhs, x, start, stop):
-        for a in range(0, x[2] - x[1], 512):
-            b = min(x[2] - x[1], a + 512)
-            mm(sub(acc, a, b), lhs, sub(x, a, b), start, stop)
-
-    def sum2(k):
-        if PEC:
-            psum(PY, ID, sub(Y, XC + k * V, XC + (k + 1) * V), True, False)
-            psum(PY, ID, sub(X, XC + k * V, XC + (k + 1) * V), False, True)
-
-    def sign2(k):
-        if PEC:
-            act(("bits", KV + k * V, KV + (k + 1) * V), PY, bias=col(SG + k), func=ACT.Sign)
-        else:
-            act(PY, sub(Y, XC + k * V, XC + (k + 1) * V), bias=col(SG + 2 + k), scale=-1.0)
-
-    def cmp2(k):
-        if not PEC:
-            vtt(("bits", KV + k * V, KV + (k + 1) * V), sub(X, XC + k * V, XC + (k + 1) * V), PY, ALU.is_ge)
-
-    vts(("inv16", 0, 256), ("invf", 0, 256), 0.25, ALU.add)
-    for k in range(2):
-        act(sub(Y, XC + k * V, XC + (k + 1) * V), T1, off=cul(1, 1, k * V, (k + 1) * V), bias=col(CR + 2 + k))
-    act(G2, Y, off=("inv16", 88, 128))
-    cut = KV - XV
-    for a, b in ((0, min(cut, V)), (V, cut)):
-        if b > a:
-            act(sub(X, XC + a, XC + b), T1, off=cul(1, 0, a, b), bias=col(CR + 2 + a // V))
-    for a, b in ((cut, V), (max(cut, V), KV)):
-        if b > a:
-            vts(sub(X, XC + a, XC + b), T1, col(CR + 2 + a // V), ALU.add, off=cul(1, 0, a, b))
-    vtt(("invf", 256, 512), ("invf", 256, 512), ("invf", 512, 768), ALU.add)
-    vgt(G2, Y, ("inv16", 216, 256), G2, ALU.max)
-    vts(("inv16", 256, 512), ("invf", 256, 512), 0.25, ALU.add)
-    vgt(G2, X, ("inv16", 256 + 88, 256 + 128), G2, ALU.max)
-    vgt(G2, X, ("inv16", 256 + 216, 512), G2, ALU.max)
-    exchange(2, G2, LAND[0], up, down)
-    sum2(0)
-    act(OM, Y, off=("inv16", 0, 88))
-    act(OC, Y, off=("inv16", 128, 216))
-    act(G0, OC, off=SN1)
-    gfill(WA2)
-    after("y", "snt2")
-    zero_by_dma("rz", [WL, WR], WB2)
-    vgt(OM, X, ("inv16", 256, 256 + 88), OM, ALU.max)
-    vgt(OM, X, ("inv16", 256 + 128, 256 + 216), OM, ALU.max)
-    act(PX, OM)
-    vst(OC, SN1, G0, LAND[0], ALU.max)
-
-    for a, b in cuts:
-        vtt(sub(PX, a, b), sub(OC, a, b), sub(PX, a, b), ALU.max)
-        act(sub(PX, a, b), sub(PX, a, b), bias=col(TH), scale=-1.0)
-    for a, b in cuts:
-        vtt(("bits", a, b), sub(S1, a, b), sub(PX, a, b), ALU.is_ge)
     votes(0, 0, PV0)
-    vtt(("bits", V, KV), sub(S1, V, KV), PX, ALU.is_ge)
+    vtt(("bits", V, V + 1024), sub(S1, V, V + 1024), sub(PA, 0, 1024), ALU.is_ge)
+    vts(PV0, PV0, 32767.0, ALU.is_ge)
+    vtt(("bits", V + 1024, KV), sub(S1, V + 1024, KV), sub(PA, 1024, V), ALU.is_ge)
     votes(0, 1, PV1)
-    E0, E1 = slot(0), slot(1)
-    sign2(0)
-    act(E0, TOP, scale=col(W2))
-    act(E1, TOP, scale=col(W2 + 1))
-    lists_first(0, 32767.0, -30720.0)
-    if PEC:
-        votes(1, 0, PV0)
-        sum2(1)
-    lists_places(0)
-    lists_second(0)
-    if PEC:
-        lists_first(1, 0.0, 2048.0)
-    else:
-        cmp2(0)
-        votes(1, 0, PV0)
+    act(("bits", KV, KV + V), PB, bias=col(SG), func=ACT.Sign)
+    act(E1, TOP, scale=col(RT + 1))
+    lists(0, -30720.0)
+    votes(1, 0, PV0)
+    gfill(half(WA1, 0))
 
     A = [slot(2), slot(3)]
-    B = [slot(10), slot(11)]
+    B = [("bits", 0, V), slot(11)]
     P = [slot(12), slot(13)]
-    for h in range(2):
-        for a in range(0, V, CHF):
-            act(sub(A[h], a, a + CHF), TF0, off=fl_("c16", 0, h, 0, a, a + CHF), scale=col(WA + h))
-            vgt(sub(P[h], a, a + CHF), TF0, fl_("c16", 0, h, 1, a, a + CHF), sub(A[h], a, a + CHF), ALU.mult)
-        if h == 0 and PEF:
-            psum(PX, ID, P[0], True, False)
+    for h, a, b in ((0, 0, 192), (0, 192, 704), (0, 704, V), (1, 0, 704), (1, 704, V)):
+        act(sub(A[h], a, b), TF0, off=fl_("c16", 0, h, 0, a, b), scale=col(WA + h))
+        vgt(sub(P[h], a, b), TF0, fl_("c16", 0, h, 1, a, b), sub(A[h], a, b), ALU.mult)
+        if h == 0 and b == V:
+            pesum(PA, ID, [P[0]])
     act(G0, P[0], off=SN1)
-    vgt(G1, P[1], SN1, G0, ALU.add)
-    exchange(4, G1, sub(TF1, ZC + V, ZC + W), down, up)
-    sign2(1)
-    if PEC:
-        votes(1, 1, PV1)
-    if PEF:
-        psum(PX, ID, P[1], False, True)
-        act(B[0], TF0, off=fl_("c16", 0, 0, 1), scale=fwc(0))
-        act(sub(TF1, ZC, ZC + V), PX)
-    else:
-        act(PX, P[0])
-        act(B[0], TF0, off=fl_("c16", 0, 0, 1), scale=fwc(0))
-    vcopy(("z16", 0, 352), ("cm", 0, 352))
-    if not PEC:
-        cmp2(1)
-        votes(1, 1, PV1)
-        lists_first(1, 32767.0, -30720.0)
-    lists_places(1)
-    if not PEF:
-        vtt(sub(TF1, ZC, ZC + V), P[1], PX, ALU.add)
-    lists_second(1)
-    vcopy(("z16", 352, 704), ("cm", 0, 352))
-    if not THREE2:
-        act(PY, TOP)
-    act(IDS, ID, scale=1.0 / KS)
+    for a, b in PARTS[4]:
+        vgt(sub(G1, a, b), P[1], sub(SN1, a // 16, b // 16), sub(G0, a, b), ALU.add)
+    exchange(4, G1, sub(TF1, ZC + V, ZC + W), down, up, PARTS[4])
+    act(("bits", KV + V, 2 * KV), XK1, bias=col(SG + 1), func=ACT.Sign)
+    votes(1, 1, PV1)
+    vts(PV0, PV0, 0.0, ALU.is_ge)
+    differences(1)
+    vtt(sub(TF1, ZC, ZC + V), P[1], PA, ALU.add)
+    lists(1, 2048.0)
+    pesum(PB, ID, [TOP])
+    gfill(half(WA1, 1))
+    gfill(half(WB1, 0))
+    gfill(half(WB1, 1))
+    act(B[0], TF0, off=fl_("c16", 0, 0, 1), scale=KS * KS)
+    IDT, IDB = ("zs", 0, 128), ("bits", V, V + 128)
+    act(IDB, ID)
+    act(IDS, ID, scale=col(W0))
+    act(IDT, ID, scale=col(W2))
 
     GA = [slot(4), slot(5)]
     VB1, VB2, VR, RA, VA = slot(6), slot(7), slot(8), slot(9), slot(12)
-    O1, YA, YB = slot(13), slot(0), slot(1)
-    halves = lambda w, a, b: [sub(w, a, b), sub(w, W + a, W + b)]
-
-    def late(acc, lhs, w, start):
-        for a, b in cuts:
-            mm(sub(acc, a, b), lhs, sub(w, a, b), start, False)
-            mm(sub(acc, a, b), lhs, sub(w, W + a, W + b), False, True)
-
-    def chain(acc, terms, out, parts):
-        for a, b in parts:
-            for x in terms[:-1]:
-                vtt(sub(acc, a, b), sub(x, a, b), sub(acc, a, b), ALU.add)
-            vtt(sub(out, a, b), sub(terms[-1], a, b), sub(acc, a, b), ALU.add)
-
-    two = [(0, 1024), (1024, V)] if SPLIT else [(0, V)]
-    vgt(VB1, TF1, fl_("c16", 1, 0, 1), E0, ALU.mult)
+    O1, YA, YB = slot(13), slot(10), slot(1)
+    vgt(VB1, TF1, fl_("c16", 1, 0, 1), TOP, ALU.mult)
     act(GA[0], TF1, off=fl_("c16", 1, 0, 0), scale=col(W2))
-    if THREE2:
-        WC2 = WA1
-        sscat(WB2, fl_("z16", 1, 0, 0), VB1)
-        vst(WA2, fl_("z16", 1, 0, 1), TOP, GA[0], ALU.mult)
-        vgt(VB2, TF1, fl_("c16", 1, 1, 1), E1, ALU.mult)
-        act(RA, WA2, off=fl_("z16", 1, 1, 1))
-        sscat(WC2, fl_("z16", 1, 1, 0), VB2)
-        vgt(VA, TF1, fl_("c16", 1, 1, 0), E1, ALU.mult)
-        vst(WA2, fl_("z16", 1, 1, 1), RA, VA, ALU.add)
-        psum(PG, ID, sub(WB2, V, W), True, False)
-        psum(PG, ID, sub(WB2, W + V, 2 * W), False, True)
-        psum(PX, ID, sub(WB2, 0, V), True, False)
-        psum(PX, ID, sub(WB2, W, W + V), False, False)
-        late(PX, ID, WC2, False)
-        chain(PG, halves(WC2, V, W) + halves(WA2, V, W), G3, [(0, GH)])
-        exchange(5, G3, LAND[1], up, down)
-        gfill(WA1)
-        act(GA[1], TF1, off=fl_("c16", 1, 1, 0), scale=col(W2 + 1))
-        own2 = halves(WA2, 0, V)
-    else:
-        vgt(VB2, TF1, fl_("c16", 1, 1, 1), E1, ALU.mult)
-        sscat(WB2, fl_("z16", 1, 0, 0), VB1)
-        vst(WA2, fl_("z16", 1, 0, 1), TOP, GA[0], ALU.mult)
-        act(GA[1], TF1, off=fl_("c16", 1, 1, 0), scale=col(W2 + 1))
-        vgt(VR, WB2, fl_("z16", 1, 1, 0), VB2, ALU.add)
-        act(RA, WA2, off=fl_("z16", 1, 1, 1))
-        vtt(VA, GA[1], PY, ALU.mult)
-        sscat(WB2, fl_("z16", 1, 1, 0), VR)
-        vst(WA2, fl_("z16", 1, 1, 1), RA, VA, ALU.add)
-        act(PG, sub(WB2, V, W))
-        chain(PG, halves(WA2, V, W) + [sub(WB2, W + V, 2 * W)], G3, [(0, GH)])
-        exchange(5, G3, LAND[1], up, down)
-        if PE2:
-            late(PX, ID, WB2, True)
-            own2 = halves(WA2, 0, V)
-        else:
-            act(PX, sub(WB2, 0, V))
-            own2 = halves(WA2, 0, V) + [sub(WB2, W, W + V)]
-    WC1 = WB2
-    act(PY, B[0])
-    act(B[1], TF0, off=fl_("c16", 0, 1, 1), scale=fwc(1))
-    if YH:
-        vgt(sub(YA, 0, YH), TF1, fl_("c16", 1, 0, 1, 0, YH), sub(GA[0], 0, YH), ALU.mult)
-    chain(PX, own2, O1, two)
-    if THREE1 and ZG:
-        gfill(WC1)
-    elif THREE1:
-        after("y", "snt5")
-        zero_by_dma("zc", [WC1], WB1)
-    act(G0, O1, off=SN1)
-    vgt(sub(YA, YH, V), TF1, fl_("c16", 1, 0, 1, YH, V), sub(GA[0], YH, V), ALU.mult)
-    dmas("y", "yia", [(T.yi[:], ap(YA), [YA], [("yi", 0, V)])])
-    vst(O1, SN1, G0, LAND[1], ALU.add)
+    sscat(WB2, fl_("z16", 1, 0, 0), VB1)
+    vst(WA2, fl_("z16", 1, 0, 1), TOP, GA[0], ALU.mult)
+    vgt(VB2, TF1, fl_("c16", 1, 1, 1), E1, ALU.mult)
+    act(GA[1], TF1, off=fl_("c16", 1, 1, 0), scale=col(W2 + 1))
+    vgt(VR, WB2, fl_("z16", 1, 1, 0), VB2, ALU.add)
+    act(RA, WA2, off=fl_("z16", 1, 1, 1))
+    vtt(VA, GA[1], PB, ALU.mult)
+    pesum(PB, IDB, [B[0]])
+    sscat(WB2, fl_("z16", 1, 1, 0), VR)
+    vst(WA2, fl_("z16", 1, 1, 1), RA, VA, ALU.add)
 
-    O0 = slot(14)
-    vtt(VB1, O1, PY, ALU.mult)
-    act(PX, O1)
-    sscat(WB1, fl_("z16", 0, 0, 0), VB1)
+    def ghosts_home(i, wa, wb, scale):
+        act(PG, sub(wb, V, W), scale=scale)
+        act(G2, sub(wb, W + V, 2 * W), scale=scale)
+        for p, q in PARTS[i]:
+            for x, o in ((sub(wa, V, W), PG), (sub(wa, W + V, 2 * W), PG), (G2, G1)):
+                for a, b in ((p, (p + q) // 2), ((p + q) // 2, q)):
+                    vtt(sub(o, a, b), sub(x, a, b), sub(PG, a, b), ALU.add)
+        exchange(i, G1, sub(LAND[i - 4], XC, LW), up, down, PARTS[i])
+
+    def own_and_home(acc, wa, land, m, out, parts, lag, each):
+        for a, b in banks:
+            vtt(sub(acc, a, b), sub(wa, a, b), sub(acc, a, b), ALU.add)
+        for a, b, e in parts:
+            vtt(sub(O_[0] if e == "v" else acc, a, b), sub(wa, W + a, W + b), sub(acc, a, b), ALU.add)
+        for a, b, e in parts:
+            if e == "s":
+                act(sub(RA, a, b), land, off=home(m, a, b))
+        for j, (a, b, e) in enumerate(parts):
+            if e == "v":
+                vgt(sub(out, a, b), land, home(m, a, b), sub(O_[0], a, b), ALU.add)
+            else:
+                vtt(sub(out, a, b), sub(RA, a, b), sub(acc, a, b), ALU.add)
+            if j >= lag:
+                each(j - lag, *parts[j - lag][:2])
+        for j in range(len(parts) - lag, len(parts)):
+            each(j, *parts[j][:2])
+
+    O_ = [VR]
+    ghosts_home(5, WA2, WB2, col(W2))
+    pesum(PA, IDT, [sub(WB2, 0, V), sub(WB2, W, W + V)])
+    vgt(YA, TF1, fl_("c16", 1, 0, 1), GA[0], ALU.mult)
+    act(B[1], TF0, off=fl_("c16", 0, 1, 1), scale=col(RT))
+    sscat(WS0, PM0, sub(IOTA, 0, GH))
+    deal("ex0", ("invf", 640, 768), WS0, 1)
+
+    own_and_home(PA, WA2, LAND[1], 1, O1, HOME1, 1,
+                 lambda j, a, b: vtt(sub(VB1, a, b), sub(O1, a, b), sub(PB, a, b), ALU.mult))
+    pesum(PA, ID, [O1])
+    for a, b in SC1:
+        sscat(WB1, fl_("z16", 0, 0, 0, a, b), sub(VB1, a, b))
     vst(WA1, fl_("z16", 0, 0, 1), O1, A[0], ALU.mult)
-    vtt(VB2, B[1], PX, ALU.mult)
+    if RBS:
+        act(sub(VB2, 0, RBS), WB1, off=fl_("z16", 0, 1, 0, 0, RBS))
+        vtt(sub(PB, 0, RBS), sub(B[1], 0, RBS), sub(PA, 0, RBS), ALU.mult)
+    if RBS < V:
+        vtt(sub(VB2, RBS, V), sub(B[1], RBS, V), sub(PA, RBS, V), ALU.mult)
     act(RA, WA1, off=fl_("z16", 0, 1, 1))
-    if THREE1:
-        sscat(WC1, fl_("z16", 0, 1, 0), VB2)
-        last = WC1
-        psum(PG, IDS, sub(WB1, V, W), True, False)
-        psum(PG, IDS, sub(WB1, W + V, 2 * W), False, True)
-        psum(PY, IDS, sub(WB1, 0, V), True, False)
-        psum(PY, IDS, sub(WB1, W, W + V), False, not PE1)
-    else:
-        vgt(VR, WB1, fl_("z16", 0, 1, 0), VB2, ALU.add)
-        sscat(WB1, fl_("z16", 0, 1, 0), VR)
-        last = WB1
-    vtt(VA, A[1], PX, ALU.mult)
+    if RBS < V:
+        vgt(sub(VR, RBS, V), WB1, fl_("z16", 0, 1, 0, RBS, V), sub(VB2, RBS, V), ALU.add)
+    if RBS:
+        vtt(sub(VR, 0, RBS), sub(VB2, 0, RBS), sub(PB, 0, RBS), ALU.add)
+    sscat(WB1, fl_("z16", 0, 1, 0), VR)
+    vtt(VA, A[1], PA, ALU.mult)
     vst(WA1, fl_("z16", 0, 1, 1), RA, VA, ALU.add)
-    act(G2 if THREE1 else PG, sub(last, V, W), scale=1.0 / KS)
-    act(G3, sub(last, W + V, 2 * W), scale=1.0 / KS)
-    own1 = halves(WA1, 0, V)
-    if PE1:
-        late(PY, IDS, last, not THREE1)
-    else:
-        act(VR if THREE1 else PY, sub(last, 0, V), scale=1.0 / KS)
-        act(VB1, sub(last, W, W + V), scale=1.0 / KS)
-        own1 = own1 + ([VR] if THREE1 else []) + [VB1]
-    chain(PG, halves(WA1, V, W) + ([G2] if THREE1 else []) + [G3], G1, [(0, GH)])
-    exchange(6, G1, LAND[2], up, down)
-    if YH1:
-        vgt(sub(YB, 0, YH1), TF1, fl_("c16", 1, 1, 1, 0, YH1), sub(GA[1], 0, YH1), ALU.mult)
-        dmas("g", "yib", [(T.yi[:, 0:YH1], ap(sub(YB, 0, YH1)), [sub(YB, 0, YH1)], [("yi", 0, YH1)])], accum_op=ALU.add)
-    chain(PY, own1, O0, two)
-    act(G0, O0, off=SN0)
-    if YH1 < V:
-        vgt(sub(YB, YH1, V), TF1, fl_("c16", 1, 1, 1, YH1, V), sub(GA[1], YH1, V), ALU.mult)
-        dmas("g", "yic", [(T.yi[:, YH1:V], ap(sub(YB, YH1, V)), [sub(YB, YH1, V)], [("yi", YH1, V)])], accum_op=ALU.add)
-    vst(O0, SN0, G0, LAND[2], ALU.add)
-    dmas("y", "yo", [(T.yo[:], ap(O0), [O0], [("yo", 0, V)])])
+    ghosts_home(6, WA1, WB1, col(W0))
+    pesum(PB, IDS, [sub(WB1, 0, V), sub(WB1, W, W + V)])
+    vts(home(0, 0, V), ("invf", 640, 728), 0.25, ALU.add)
+    if YS:
+        act(sub(PA, V - YS, V), sub(GA[1], V - YS, V))
+        act(sub(YB, V - YS, V), TF1, off=fl_("c16", 1, 1, 1, V - YS, V))
+    if YS < V:
+        act(sub(PA, 0, V - YS), sub(YA, 0, V - YS))
+        vgt(sub(YB, 0, V - YS), TF1, fl_("c16", 1, 1, 1, 0, V - YS), sub(GA[1], 0, V - YS), ALU.mult)
+    if YS:
+        vtt(sub(PA, V - YS, V), sub(YB, V - YS, V), sub(PA, V - YS, V), ALU.mult)
+    if YS < V:
+        vtt(sub(YB, 0, V - YS), sub(YB, 0, V - YS), sub(PA, 0, V - YS), ALU.add)
+    if YS:
+        vtt(sub(YB, V - YS, V), sub(YA, V - YS, V), sub(PA, V - YS, V), ALU.add)
+    dmas("y", "yib", [(T.yi[:], ap(YB), [YB], [("yi", 0, V)])])
+    O0 = slot(14)
+    own_and_home(PB, WA1, LAND[2], 0, O0, HOME0, 0,
+                 lambda j, a, b: dmas("y", "yo%d" % j, [(T.yo[:, a:b], ap(sub(O0, a, b)), [sub(O0, a, b)], [("yo", a, b)])]))
     for sem in total:
         after("g", sem)

from concourse.mybir import dt, AluOpType as ALU, ActivationFunctionType as ACT

V, GH, KV, W = 1408, 640, 2816, 2048
SL = 1424
NSL = 15
ZC = 16
XC = 32
LW = XC + GH
KS = float(2 ** 24)

SCRATCH = {
    "w0": ("sbuf", [128, 4096], "float32"), "w1": ("sbuf", [128, 4096], "float32"),
    "w2": ("sbuf", [128, 4096], "float32"), "w3": ("sbuf", [128, 4096], "float32"),
    "pool": ("sbuf", [128, NSL * SL], "float32"),
    "t0": ("sbuf", [128, W], "float32"), "t1": ("sbuf", [128, W], "float32"),
    "tf0": ("sbuf", [128, W + ZC], "bfloat16"), "tf1": ("sbuf", [128, W + ZC], "float32"),
    "cli": ("sbuf", [128, V], "int32"), "cui": ("sbuf", [128, 704], "int32"), "cm": ("sbuf", [128, 704], "int32"),
    "fz": ("sbuf", [128, V], "int32"), "dz": ("sbuf", [128, 704], "float32"),
    "sni": ("sbuf", [128, 80], "int32"), "cri": ("sbuf", [128, 4], "int32"), "thi": ("sbuf", [128, 4], "int32"),
    "snm": ("sbuf", [128, 160], "int32"),
    "fwf": ("sbuf", [128, 4], "float32"), "col": ("sbuf", [128, 32], "float32"),
    "sn16": ("sbuf", [128, 160], "uint16"), "cu16": ("sbuf", [128, 704], "uint16"), "pm16": ("sbuf", [128, 352], "uint16"),
    "invf": ("sbuf", [128, 768], "float32"), "inv16": ("sbuf", [128, 704], "uint16"),
    "c16": ("sbuf", [128, 704], "uint16"), "z16": ("sbuf", [128, 704], "uint16"),
    "sm": ("sbuf", [128, 448], "float32"), "zs": ("sbuf", [128, 256], "float32"),
    "land": ("sbuf", [128, 3 * LW], "float32"), "gs": ("sbuf", [128, 3 * GH], "float32"), "gfl": ("sbuf", [128, GH], "bfloat16"),
    "bits": ("sbuf", [128, 2 * KV], "bfloat16"),
    "ident": ("sbuf", [128, 256], "float32"), "band": ("sbuf", [128, 2 * 160], "bfloat16"), "bsrc": ("sbuf", [128, 16], "bfloat16"),
    "ps": ("psum", [128, 4096], "float32"),
}
DMAS = ["snd", "cul", "cur", "cua", "cl", "cr", "fl", "fu", "fw", "top", "zl", "zr", "z1", "z0", "exl", "exr", "ex1", "ex0",
        "add", "yia", "yib"] + ["yo%d" % i for i in range(6)]
SEMAPHORES = ["cv", "cs", "cp", "cg"] + ["d" + n for n in DMAS] + ["arr%d" % i for i in range(7)] + ["snt%d" % i for i in range(7)]

ZV = 2048
PRE_S = 2112
PRE_V = 1120
RV = 1920
YV, XV = 1408, 1408
RBS = 1056
EARLY = True
YS = 896
WHOLE, HALVES = ((0, GH),), ((0, GH // 2), (GH // 2, GH))
PARTS = [WHOLE, WHOLE, HALVES, WHOLE, WHOLE, HALVES, HALVES]
HOMEC = [(0, 192), (192, 512), (512, 960), (960, 1408)]
L1A = 352
HOME1 = [(0, 352, "v"), (352, 704, "s"), (704, 1056, "s"), (1056, 1408, "s")]
SC1 = [(0, 352), (352, 704), (704, 1408)]
HOME0 = [(0, 192, "s"), (192, 608, "s"), (608, 1024, "s"), (1024, 1408, "s")]


def rank_program(g, core, T, topo):
    rank = T.rank_of(core)
    if rank is None:
        return
    n = len(T.cores)
    down, up = T.cores[(rank - 1) % n], T.cores[(rank + 1) % n]
    Q = {"v": g.vector, "s": g.scalar, "p": g.tensor, "g": g, "y": g.sync}
    CNT = {"v": "cv", "s": "cs", "p": "cp", "g": "cg"}
    total, known, log = {}, {q: {} for q in Q}, {}

    def ap(r):
        if len(r) == 4:
            return T[r[0]][:, r[1]:r[2]:r[3]]
        return T[r[0]][:, r[1]:r[2]]

    def need(q, reads, writes):
        toks = {}
        for rs, wr in ((reads, False), (writes, True)):
            for r in rs:
                for (lo, hi, w, eng, sem, val) in log.get(r[0], []):
                    hit = lo < r[2] and r[1] < hi
                    if eng == q:
                        must = hit and ((w and not wr) or (q != "p" and (w or wr)))
                    elif r[0] == "ps":
                        must = lo // 512 <= (r[2] - 1) // 512 and r[1] // 512 <= (hi - 1) // 512
                    else:
                        lo4, hi4 = lo // 8 * 8, (hi + 7) // 8 * 8
                        must = (hit and (w or wr)) or (w and wr and lo4 < r[2] and r[1] < hi4)
                    if must:
                        toks[sem] = max(toks.get(sem, 0), val)
        for sem, val in toks.items():
            if known[q].get(sem, 0) < val:
                Q[q].wait_ge(T.sem[sem], val)
                known[q][sem] = val

    def note(eng, reads, writes, sem, val):
        for rs, wr in ((reads, False), (writes, True)):
            for r in rs:
                log.setdefault(r[0], []).append((r[1], r[2], wr, eng, sem, val))

    def op(q, call, reads, writes):
        need(q, reads, writes)
        sem = CNT[q]
        total[sem] = total.get(sem, 0) + 1
        call().then_inc(T.sem[sem], 1)
        note(q, reads, writes, sem, total[sem])

    def dmas(q, name, items, **kw):
        sem = "d" + name
        for it in items:
            need(q, it[2], it[3])
        for it in items:
            Q[q].dma_start(it[0], it[1], **kw).then_inc(T.sem[sem], 16)
        total[sem] = 16 * len(items)
        for it in items:
            note("dma", it[2], it[3], sem, total[sem])

    def load(q, name, o, src):
        dmas(q, name, [(ap(o), src, [], [o])])

    def after(q, sem):
        if known[q].get(sem, 0) < total[sem]:
            Q[q].wait_ge(T.sem[sem], total[sem])
            known[q][sem] = total[sem]

    def exchange(i, src, dst, to, frm, parts=((0, GH),)):
        rid, pid, _se = topo.addr(to)
        for a, b in parts:
            need("g", [sub(src, a, b)], [])
            g.remote_dma(ap(sub(dst, a, b)), ap(sub(src, a, b)), T.sem["arr%d" % i], T.sem["snt%d" % i], pid, rid, topo.mask(core, to))
        total["snt%d" % i] = len(parts) * len(topo.engines(core, to))
        total["arr%d" % i] = len(parts) * len(topo.engines(frm, core))
        note("dma", [src], [], "snt%d" % i, total["snt%d" % i])
        note("dma", [], [dst], "arr%d" % i, total["arr%d" % i])

    def sub(r, a, b):
        return (r[0], r[1] + a, r[1] + b)

    def slot(i, a=0, b=V):
        return ("pool", i * SL + a, i * SL + b)

    def cl_(x):
        return ap(x) if isinstance(x, tuple) else x

    def rd(*xs):
        return [x for x in xs if isinstance(x, tuple)]

    def ind(win, off):
        return ap(win).indirect(ap(off))

    def vcopy(o, i):
        op("v", lambda: g.vector.tensor_copy(ap(o), ap(i)), [i], [o])

    def vset(o, c):
        op("v", lambda: g.vector.memset(ap(o), c), [], [o])

    def vts(o, i, s1, o0, s2=None, o1=None, off=None):
        src = (lambda: ap(i)) if off is None else (lambda: ind(i, off))
        if o1 is None:
            op("v", lambda: g.vector.tensor_scalar(ap(o), src(), cl_(s1), None, o0), rd(i, s1, off), [o])
        else:
            op("v", lambda: g.vector.tensor_scalar(ap(o), src(), cl_(s1), cl_(s2), o0, o1), rd(i, s1, s2, off), [o])

    def vtt(o, a, b, alu):
        op("v", lambda: g.vector.tensor_tensor(ap(o), ap(a), ap(b), alu), [a, b], [o])

    def vgather(o, win, off):
        op("v", lambda: g.vector.tensor_copy(ap(o), ind(win, off)), [win, off], [o])

    def vgt(o, win, off, b, alu):
        op("v", lambda: g.vector.tensor_tensor(ap(o), ind(win, off), ap(b), alu), [win, off, b], [o])

    def vscat(win, off, i):
        op("v", lambda: g.vector.tensor_copy(ind(win, off), ap(i)), [i, off], [win])

    def vst(win, off, a, b, alu):
        op("v", lambda: g.vector.tensor_tensor(ind(win, off), ap(a), ap(b), alu), [a, b, off], [win])

    def act(o, i, off=None, bias=None, scale=None, func=None):
        kw = {}
        if bias is not None:
            kw["bias"] = cl_(bias)
        if scale is not None:
            kw["scale"] = cl_(scale)
        f = func if func is not None else (ACT.Copy if bias is None else ACT.Identity)
        src = (lambda: ap(i)) if off is None else (lambda: ind(i, off))
        op("s", lambda: g.scalar.activation(ap(o), src(), f, **kw), rd(i, off, bias, scale), [o])

    def sscat(win, off, i):
        op("s", lambda: g.scalar.activation(ind(win, off), ap(i), ACT.Silu), [i, off], [win])

    def gfill(o, step=0, base=0):
        op("g", lambda: g.iota(ap(o), [[step, o[2] - o[1]]], base, 0, allow_small_or_imprecise_dtypes=True), [], [o])

    def mm(o, lhs, rhs, start, stop):
        op("p", lambda: g.tensor.matmul(ap(o), ap(lhs), ap(rhs), start, stop), [lhs, rhs], [o])

    def pesum(acc, lhs, xs):
        width = xs[0][2] - xs[0][1]
        for a in range(0, width, 512):
            b = min(width, a + 512)
            for j, x in enumerate(xs):
                mm(sub(acc, a, b), lhs, sub(x, a, b), j == 0, j == len(xs) - 1)

    ONE = (slice(0, 128, 18), slice(14, 126, 14))

    def zero_one(name, win, s):
        z = ("zs", 0, (win[2] - win[1]) // 16)
        dmas("y", name, [(T[win[0]][ONE[s], win[1]:win[2]], ap(z), [z], [win])])

    def deal(name, tile, win, s):
        dmas("y", name, [(ap(tile), T[win[0]][ONE[s], win[1]:win[2]], [win], [tile])])

    WL, WR, WA2, WB2 = (("w%d" % i, 0, 4096) for i in range(4))
    WA1, WB1 = WL, WR
    T0, T1, TF0, TF1 = ("t0", 0, W), ("t1", 0, W), ("tf0", 0, W + ZC), ("tf1", 0, W + ZC)
    WS1, WS0 = sub(WA2, 0, W), T0
    SN0, SN1, PM0, PM1 = (("sn16", 40 * i, 40 * i + 40) for i in range(4))
    PA, PB, PG = ("ps", 0, V), ("ps", 1536, 1536 + V), ("ps", 3072, 3072 + GH)
    PV0, PV1, PT = ("ps", 3072, 3160), ("ps", 3584, 3672), ("ps", 3200, 3552)
    G0, G1, G2 = (("gs", i * GH, (i + 1) * GH) for i in range(3))
    LAND = [("land", i * LW, (i + 1) * LW) for i in range(3)]
    col = lambda i: ("col", i, i + 1)
    CR, TH, SG, WA, W2 = 0, 4, 8, 12, 16
    W0, RC, RT = 20, 24, 28
    IOTA, AL, S1 = slot(0, 0, KV), slot(2, 0, KV), slot(4, 0, KV)
    X, Y, OC, OM, TOP = slot(6, 0, KV + XC), slot(8, 0, KV + XC), slot(10), slot(11), slot(14)
    ID, IDS = ("ident", 0, 128), ("ident", 128, 256)
    banks = [(a, min(V, a + 512)) for a in range(0, V, 512)]
    cul = lambda m, s, a, b: ("cu16", (m * 2 + s) * 176 + a // 16, (m * 2 + s) * 176 + b // 16)
    fl_ = lambda name, m, h, s, a=0, b=V: (name, ((m * 2 + h) * 2 + s) * 88 + a // 16, ((m * 2 + h) * 2 + s) * 88 + b // 16)
    inv = lambda s, a, b: ("inv16", s * 256 + a // 16, s * 256 + b // 16)
    home = lambda m, a, b: ("inv16", 512 + m * 96 + a // 16, 512 + m * 96 + b // 16)
    half = lambda w, j: sub(w, j * W, (j + 1) * W)

    load("s", "snd", ("sni", 0, 80), T.snd[:])
    load("y", "cul", ("cui", 352, 528), T.cu[:, 352:528])
    load("y", "cl", ("cli", 0, V), T.cl[:])
    load("s", "cur", ("cui", 528, 704), T.cu[:, 528:704])
    load("s", "cua", ("cui", 0, 352), T.cu[:, 0:352])
    dmas("s", "cr", [(T.cri[:], T.cr[:], [], [("cri", 0, 4)]), (T.thi[:, 0:2], T.th[:], [], [("thi", 0, 2)]),
                     (T.fwf[:], T.fw[:], [], [("fwf", 0, 4)])])
    gfill(sub(IOTA, 0, 352), 1, XC)
    vset(("zs", 0, 256), 0.0)
    zero_one("zr", WR, 1)
    zero_one("z1", WS1, 0)
    gfill(sub(IOTA, 704, V), 1, XC + 704)
    gfill(sub(IOTA, V, KV), 1, XC + V)
    vset(sub(WL, 0, ZV), 0.0)
    act(sub(IOTA, 352, 704), sub(IOTA, 0, 352), bias=352.0, func=ACT.Silu)
    act(sub(WL, 3072, 4096), sub(WL, 0, 1024))

    def dealt(out, src, tmp, bits):
        k = src[2] - src[1]
        vts(sub(tmp, 0, k), src, float(2 ** (bits + 4) + 1), ALU.mult)
        vts(sub(tmp, k, 2 * k), sub(tmp, 0, k), 4, ALU.logical_shift_right, 2 ** (bits + 4) - 1, ALU.bitwise_and)
        vcopy(out, sub(tmp, k, 2 * k))

    vcopy(("sn16", 0, 80), ("sni", 0, 80))
    dealt(("pm16", 0, 176), ("cui", 352, 528), ("cm", 0, 352), 8)
    vset(sub(WL, ZV, 3072), 0.0)
    vset(ID, 1.0)
    for a, b in PARTS[0]:
        vgather(sub(G0, a, b), ("cli", 0, V), sub(SN0, a // 16, b // 16))
    exchange(0, G0, sub(T0, V, W), down, up, PARTS[0])
    op("g", lambda: g.affine_select(ap(ID), ap(ID), [[-1, 128]], ALU.is_equal, 0.0, 0, 1), [ID], [ID])
    for x in [("tf0", 0, ZC), ("tf1", 0, ZC), sub(X, 0, XC), sub(Y, 0, XC), ("band", 0, 320)] + [sub(x, 0, XC) for x in LAND]:
        gfill(x)
    gfill(("bsrc", 0, 8), 0, 4096)
    gfill(half(WB2, 0))
    dmas("g", "top", [(ap(TOP), T.top[:], [], [TOP])])
    if not EARLY:
        after("y", "snt0")
    load("y", "fu", ("fz", 0, V), T.fu[:])
    load("y", "fl", ("tf0", ZC, ZC + V), T.fl[:])
    sscat(WL, ("pm16", 0, 88), sub(IOTA, 0, V))
    if PRE_S > V:
        sscat(WL, ("pm16", 88, PRE_S // 16), sub(IOTA, V, PRE_S))
    dealt(("pm16", 176, 352), ("cui", 528, 704), ("cm", 352, 704), 8)
    vcopy(sub(T0, 0, V), ("cli", 0, V))
    vts(("cm", 0, 352), ("cui", 0, 352), W - 1, ALU.bitwise_and)
    vcopy(("col", CR, CR + 4), ("cri", 0, 4))
    vcopy(("col", TH, TH + 2), ("thi", 0, 2))
    vcopy(("cu16", 0, 352), ("cm", 0, 352))
    dealt(("sn16", 80, 160), ("sni", 0, 80), ("snm", 0, 160), 7)
    op("v", lambda: g.vector.reciprocal(ap(("col", RC, RC + 2)), T.fwf[:, 0:3:2]), [("fwf", 0, 4)], [("col", RC, RC + 2)])
    vts(("col", SG + 2, SG + 4), ("col", CR + 2, CR + 4), col(TH + 1), ALU.add)
    vts(("col", WA, WA + 2), ("fwf", 0, 2), KS, ALU.mult)
    vts(col(W0), ("fwf", 0, 1), 1.0 / KS, ALU.mult)
    vts(("col", W2, W2 + 2), ("fwf", 2, 4), 1.0 / (KS * KS), ALU.mult)
    vts(("col", SG, SG + 2), ("col", SG + 2, SG + 4), -1.0, ALU.mult, 0.5, ALU.add)
    vts(col(RT), ("fwf", 1, 2), col(RC), ALU.mult, KS * KS, ALU.mult)
    vts(col(RT + 1), ("fwf", 3, 4), col(RC + 1), ALU.mult)
    vscat(WR, ("pm16", 176, 176 + PRE_V // 16), sub(IOTA, 0, PRE_V))

    for a, b in ((0, L1A), (L1A, 704), (704, V), (V, V + 704), (V + 704, KV)):
        if a == 0:
            vts(sub(AL, a, b), T0, col(CR), ALU.add, off=cul(0, 0, a, b))
        else:
            act(sub(AL, a, b), T0, off=cul(0, 0, a, b), bias=col(CR + a // V))
        vgt(sub(S1, a, b), T0, cul(0, 1, a, b), sub(AL, a, b), ALU.add)
        if b == V:
            pesum(PA, ID, [sub(S1, 0, V)])
    act(G2, sub(S1, 0, V), off=SN1)
    for a, b in PARTS[1]:
        vgt(sub(G1, a, b), sub(S1, V, KV), sub(SN1, a // 16, b // 16), sub(G2, a, b), ALU.max)
    exchange(1, G1, sub(T1, V, W), down, up, PARTS[1])
    op("g", lambda: g.affine_select(T.bsrc[:, 8:16], T.bsrc[:, 0:8], [[-16, 8]], ALU.is_ge, 0.0, 0, 1), [("bsrc", 0, 8)], [("bsrc", 8, 16)])
    for j in range(2):
        o = ("band", 160 * j + 16 + j, 160 * j + 16 + j + 113, 16)
        op("g", lambda o=o: g.affine_select(ap(o), T.bsrc[:, 8:16], [[16, 8]], ALU.is_ge, 0.0, 15, -1), [("bsrc", 8, 16)], [o])
    gfill(half(WB2, 1))
    gfill(half(WA2, 1))
    vscat(WR, ("pm16", 176 + PRE_V // 16, 176 + RV // 16), sub(IOTA, PRE_V, RV))
    if PRE_S < KV:
        sscat(WL, ("pm16", PRE_S // 16, 176), sub(IOTA, PRE_S, KV))
    deal("exl", ("invf", 0, 256), WL, 0)
    sscat(WS1, PM1, sub(IOTA, 0, GH))
    if RV < KV:
        sscat(WR, ("pm16", 176 + RV // 16, 352), sub(IOTA, RV, KV))
    deal("exr", ("invf", 256, 512), WR, 1)
    deal("ex1", ("invf", 512, 640), WS1, 0)
    zero_one("z0", WS0, 1)
    vts(("cm", 352, 704), ("cui", 352, 704), W - 1, ALU.bitwise_and)
    vtt(sub(T1, 0, V), sub(S1, V, KV), PA, ALU.max)
    vcopy(("cu16", 352, 704), ("cm", 352, 704))
    fz = lambda l, k: ("fz", l * 176 + k * 88, l * 176 + k * 88 + 88)

    def differences(m):
        for l in range(4 * m, 4 * m + 4):
            vtt(("dz", l * 88, l * 88 + 88), fz(l, 0), fz(l, 1), ALU.subtract)

    differences(0)

    def children(tab, s, nv):
        for a, b in ((0, min(V, KV - nv)), (V, KV - nv)):
            if b > a:
                act(sub(tab, XC + a, XC + b), T1, off=cul(1, s, a, b), bias=col(CR + 2 + a // V))
        for a, b in ((KV - nv, V), (max(KV - nv, V), KV)):
            if b > a:
                vts(sub(tab, XC + a, XC + b), T1, col(CR + 2 + a // V), ALU.add, off=cul(1, s, a, b))

    vts(inv(0, 0, 4096), ("invf", 0, 256), 0.25, ALU.add)
    children(Y, 1, YV)
    act(G2, Y, off=inv(0, V, W))
    children(X, 0, XV)
    vgt(G2, Y, inv(0, W + V, 2 * W), G2, ALU.max)
    vts(inv(1, 0, 4096), ("invf", 256, 512), 0.25, ALU.add)
    for a, b in PARTS[2]:
        for u in (V, W + V):
            vgt(sub(G2, a, b), X, inv(1, u + a, u + b), sub(G2, a, b), ALU.max)
    exchange(2, G2, sub(LAND[0], XC, LW), up, down, PARTS[2])
    pesum(PB, ID, [sub(Y, XC, XC + V), sub(X, XC, XC + V)])

    E1, H = slot(1), slot(12)
    act(OM, Y, off=inv(0, 0, V))
    act(OC, Y, off=inv(0, W, W + V), bias=col(TH), scale=-1.0)
    act(("gfl", 0, GH), ("tf0", ZC, ZC + V), off=SN0)
    exchange(3, ("gfl", 0, GH), sub(TF0, ZC + V, ZC + W), down, up)
    vgt(OM, X, inv(1, 0, V), OM, ALU.max)
    vts(home(1, 0, V), ("invf", 512, 600), 0.25, ALU.add)
    for a, b in banks:
        vgt(sub(OM, a, b), X, inv(1, W + a, W + b), sub(OM, a, b), ALU.max)
    XK1, YK1 = sub(X, XC + V, XC + KV), sub(Y, XC + V, XC + KV)
    dmas("g", "add", [(ap(XK1), ap(YK1), [XK1, YK1], [XK1])], accum_op=ALU.add)
    gfill(half(WA2, 0))
    for a, b in banks:
        act(sub(PA, a, b), sub(OM, a, b), bias=col(TH), scale=-1.0)
    for a, b in banks:
        vtt(sub(PA, a, b), sub(OC, a, b), sub(PA, a, b), ALU.min)
    for a, b in HOMEC:
        act(sub(H, a, b), LAND[0], off=home(1, a, b), bias=col(TH), scale=-1.0)
    for j in range(len(HOMEC) + 1):
        if j < len(HOMEC):
            vtt(sub(PA, *HOMEC[j]), sub(H, *HOMEC[j]), sub(PA, *HOMEC[j]), ALU.min)
        if j > 0:
            vtt(sub(("bits", 0, V), *HOMEC[j - 1]), sub(S1, *HOMEC[j - 1]), sub(PA, *HOMEC[j - 1]), ALU.is_ge)

    def votes(m, k, out):
        for i in range(16):
            j = i % 2
            a = 160 * j + 16 + j - i
            b0 = m * KV + k * V
            mm(out, ("band", a, a + 128), ("bits", b0 + i, b0 + V - 15 + i, 16), i == 0, i == 15)

    def lists(m, off):
        c0 = m * 352
        four = lambda name, l, a=0, k=1: (name, a + l * 88, a + (l + k) * 88)
        for l in range(4):
            vtt(four("ps", l, PT[1]), four("dz", m * 4 + l), PV0, ALU.mult)
        vts(four("sm", 4), PV0, 65536.0, ALU.mult, off, ALU.add)
        for l in range(4):
            vtt(four("cm", l), fz(m * 4 + l, 1), four("ps", l, PT[1]), ALU.add)
        vts(four("cm", 4, 0, 2), four("cm", 0, 0, 2), W - 1, ALU.bitwise_and)
        vtt(PV1, four("sm", 4), PV1, ALU.add)
        vts(four("cm", 6, 0, 2), four("cm", 2, 0, 2), W - 1, ALU.bitwise_and)
        for l in range(4):
            vtt(four("sm", l), four("cm", 4 + l), PV1, ALU.min)
            if l == 1:
                vts(four("c16", 0, c0), four("sm", 0), float(ZC), ALU.add)
        vts(four("c16", 1, c0), four("sm", 1), float(ZC), ALU.add)
        vcopy(("z16", c0, c0 + 352), ("cm", 0, 352))
        vts(four("c16", 2, c0, 2), four("sm", 2, 0, 2), float(ZC), ALU.add)

    votes(0, 0, PV0)
    vtt(("bits", V, V + 1024), sub(S1, V, V + 1024), sub(PA, 0, 1024), ALU.is_ge)
    vts(PV0, PV0, 32767.0, ALU.is_ge)
    vtt(("bits", V + 1024, KV), sub(S1, V + 1024, KV), sub(PA, 1024, V), ALU.is_ge)
    votes(0, 1, PV1)
    act(("bits", KV, KV + V), PB, bias=col(SG), func=ACT.Sign)
    act(E1, TOP, scale=col(RT + 1))
    lists(0, -30720.0)
    votes(1, 0, PV0)
    gfill(half(WA1, 0))

    A = [slot(2), slot(3)]
    B = [("bits", 0, V), slot(11)]
    P = [slot(12), slot(13)]
    for h, a, b in ((0, 0, 192), (0, 192, 704), (0, 704, V), (1, 0, 704), (1, 704, V)):
        act(sub(A[h], a, b), TF0, off=fl_("c16", 0, h, 0, a, b), scale=col(WA + h))
        vgt(sub(P[h], a, b), TF0, fl_("c16", 0, h, 1, a, b), sub(A[h], a, b), ALU.mult)
        if h == 0 and b == V:
            pesum(PA, ID, [P[0]])
    act(G0, P[0], off=SN1)
    for a, b in PARTS[4]:
        vgt(sub(G1, a, b), P[1], sub(SN1, a // 16, b // 16), sub(G0, a, b), ALU.add)
    exchange(4, G1, sub(TF1, ZC + V, ZC + W), down, up, PARTS[4])
    act(("bits", KV + V, 2 * KV), XK1, bias=col(SG + 1), func=ACT.Sign)
    votes(1, 1, PV1)
    vts(PV0, PV0, 0.0, ALU.is_ge)
    differences(1)
    vtt(sub(TF1, ZC, ZC + V), P[1], PA, ALU.add)
    lists(1, 2048.0)
    pesum(PB, ID, [TOP])
    gfill(half(WA1, 1))
    gfill(half(WB1, 0))
    gfill(half(WB1, 1))
    act(B[0], TF0, off=fl_("c16", 0, 0, 1), scale=KS * KS)
    IDT, IDB = ("zs", 0, 128), ("bits", V, V + 128)
    act(IDB, ID)
    act(IDS, ID, scale=col(W0))
    act(IDT, ID, scale=col(W2))

    GA = [slot(4), slot(5)]
    VB1, VB2, VR, RA, VA = slot(6), slot(7), slot(8), slot(9), slot(12)
    O1, YA, YB = slot(13), slot(10), slot(1)
    vgt(VB1, TF1, fl_("c16", 1, 0, 1), TOP, ALU.mult)
    act(GA[0], TF1, off=fl_("c16", 1, 0, 0), scale=col(W2))
    sscat(WB2, fl_("z16", 1, 0, 0), VB1)
    vst(WA2, fl_("z16", 1, 0, 1), TOP, GA[0], ALU.mult)
    vgt(VB2, TF1, fl_("c16", 1, 1, 1), E1, ALU.mult)
    act(GA[1], TF1, off=fl_("c16", 1, 1, 0), scale=col(W2 + 1))
    vgt(VR, WB2, fl_("z16", 1, 1, 0), VB2, ALU.add)
    act(RA, WA2, off=fl_("z16", 1, 1, 1))
    vtt(VA, GA[1], PB, ALU.mult)
    pesum(PB, IDB, [B[0]])
    sscat(WB2, fl_("z16", 1, 1, 0), VR)
    vst(WA2, fl_("z16", 1, 1, 1), RA, VA, ALU.add)

    def ghosts_home(i, wa, wb, scale):
        act(PG, sub(wb, V, W), scale=scale)
        act(G2, sub(wb, W + V, 2 * W), scale=scale)
        for p, q in PARTS[i]:
            for x, o in ((sub(wa, V, W), PG), (sub(wa, W + V, 2 * W), PG), (G2, G1)):
                for a, b in ((p, (p + q) // 2), ((p + q) // 2, q)):
                    vtt(sub(o, a, b), sub(x, a, b), sub(PG, a, b), ALU.add)
        exchange(i, G1, sub(LAND[i - 4], XC, LW), up, down, PARTS[i])

    def own_and_home(acc, wa, land, m, out, parts, lag, each):
        for a, b in banks:
            vtt(sub(acc, a, b), sub(wa, a, b), sub(acc, a, b), ALU.add)
        for a, b, e in parts:
            vtt(sub(O_[0] if e == "v" else acc, a, b), sub(wa, W + a, W + b), sub(acc, a, b), ALU.add)
        for a, b, e in parts:
            if e == "s":
                act(sub(RA, a, b), land, off=home(m, a, b))
        for j, (a, b, e) in enumerate(parts):
            if e == "v":
                vgt(sub(out, a, b), land, home(m, a, b), sub(O_[0], a, b), ALU.add)
            else:
                vtt(sub(out, a, b), sub(RA, a, b), sub(acc, a, b), ALU.add)
            if j >= lag:
                each(j - lag, *parts[j - lag][:2])
        for j in range(len(parts) - lag, len(parts)):
            each(j, *parts[j][:2])

    O_ = [VR]
    ghosts_home(5, WA2, WB2, col(W2))
    pesum(PA, IDT, [sub(WB2, 0, V), sub(WB2, W, W + V)])
    vgt(YA, TF1, fl_("c16", 1, 0, 1), GA[0], ALU.mult)
    act(B[1], TF0, off=fl_("c16", 0, 1, 1), scale=col(RT))
    sscat(WS0, PM0, sub(IOTA, 0, GH))
    deal("ex0", ("invf", 640, 768), WS0, 1)

    own_and_home(PA, WA2, LAND[1], 1, O1, HOME1, 1,
                 lambda j, a, b: vtt(sub(VB1, a, b), sub(O1, a, b), sub(PB, a, b), ALU.mult))
    pesum(PA, ID, [O1])
    for a, b in SC1:
        sscat(WB1, fl_("z16", 0, 0, 0, a, b), sub(VB1, a, b))
    vst(WA1, fl_("z16", 0, 0, 1), O1, A[0], ALU.mult)
    if RBS:
        act(sub(VB2, 0, RBS), WB1, off=fl_("z16", 0, 1, 0, 0, RBS))
        vtt(sub(PB, 0, RBS), sub(B[1], 0, RBS), sub(PA, 0, RBS), ALU.mult)
    if RBS < V:
        vtt(sub(VB2, RBS, V), sub(B[1], RBS, V), sub(PA, RBS, V), ALU.mult)
    act(RA, WA1, off=fl_("z16", 0, 1, 1))
    if RBS < V:
        vgt(sub(VR, RBS, V), WB1, fl_("z16", 0, 1, 0, RBS, V), sub(VB2, RBS, V), ALU.add)
    if RBS:
        vtt(sub(VR, 0, RBS), sub(VB2, 0, RBS), sub(PB, 0, RBS), ALU.add)
    sscat(WB1, fl_("z16", 0, 1, 0), VR)
    vtt(VA, A[1], PA, ALU.mult)
    vst(WA1, fl_("z16", 0, 1, 1), RA, VA, ALU.add)
    ghosts_home(6, WA1, WB1, col(W0))
    pesum(PB, IDS, [sub(WB1, 0, V), sub(WB1, W, W + V)])
    vts(home(0, 0, V), ("invf", 640, 728), 0.25, ALU.add)
    if YS:
        act(sub(PA, V - YS, V), sub(GA[1], V - YS, V))
        act(sub(YB, V - YS, V), TF1, off=fl_("c16", 1, 1, 1, V - YS, V))
    if YS < V:
        act(sub(PA, 0, V - YS), sub(YA, 0, V - YS))
        vgt(sub(YB, 0, V - YS), TF1, fl_("c16", 1, 1, 1, 0, V - YS), sub(GA[1], 0, V - YS), ALU.mult)
    if YS:
        vtt(sub(PA, V - YS, V), sub(YB, V - YS, V), sub(PA, V - YS, V), ALU.mult)
    if YS < V:
        vtt(sub(YB, 0, V - YS), sub(YB, 0, V - YS), sub(PA, 0, V - YS), ALU.add)
    if YS:
        vtt(sub(YB, V - YS, V), sub(YA, V - YS, V), sub(PA, V - YS, V), ALU.add)
    dmas("y", "yib", [(T.yi[:], ap(YB), [YB], [("yi", 0, V)])])
    O0 = slot(14)
    own_and_home(PB, WA1, LAND[2], 0, O0, HOME0, 0,
                 lambda j, a, b: dmas("y", "yo%d" % j, [(T.yo[:, a:b], ap(sub(O0, a, b)), [sub(O0, a, b)], [("yo", a, b)])]))
    for sem in total:
        after("g", sem)
